import numpy as np
import ml_dtypes


def mxq(x, axis, fmt="e4m3"):
    dtype, down = {"e4m3": (ml_dtypes.float8_e4m3fn, 7), "e5m2": (ml_dtypes.float8_e5m2, 14)}[fmt]
    v = np.moveaxis(np.asarray(x, np.float32).astype(ml_dtypes.bfloat16).astype(np.float64), axis, -1)
    blocks = v.reshape(v.shape[:-1] + (-1, 32))
    amax = np.abs(blocks).max(-1, keepdims=True)
    byte = np.maximum(np.where(amax > 0, np.frexp(amax)[1] - 1 + 127, 0) - down, 1)
    scale = np.exp2(byte - 127.0)
    codes = (blocks / scale).astype(np.float32).astype(dtype).astype(np.float64)
    return np.moveaxis((codes * scale).reshape(v.shape), -1, axis)


WIDE = False


def mx_kscale(k):
    if not WIDE:
        return np.ones(k)
    levels = np.array([18, -18])
    if k % 512:
        return np.exp2(np.random.permutation(np.resize(levels, k // 32))).repeat(32)
    a = np.empty((k // 512, 16))
    for p in range(k // 512):
        a[p, :8] = np.random.permutation(np.resize(levels, 8))
        for g in range(8):
            far = levels[np.abs(levels - a[p, g]) >= 10]
            a[p, g + 8] = far[np.random.randint(len(far))]
    return np.exp2(a.ravel()).repeat(32)


def f64(x):
    return np.asarray(x).astype(np.float64)


def striped(idx):
    return np.tile(np.asarray(idx).reshape(-1, 16).T, (8, 1)).astype(np.uint16)


def unstriped(offs):
    return offs[:16].T.reshape(-1).astype(np.int64)


B, N, T, D, R = 1, 512, 2048, 512, 1024


def setup_inputs():
    n = np.random.standard_normal
    idx = np.random.permutation(T)[:B * N]
    s = mx_kscale(D)[:, None]
    z = mx_kscale(R)[:, None]
    x = n((B, D, R))
    teach = np.exp(n((B, R, N)))
    teach = teach / teach.sum(-1, keepdims=True)
    return {
        "xT": (x * s).astype(np.float32),
        "wT": (n((D, T)) * (0.50 / np.sqrt(D)) / s).astype(np.float32),
        "y": teach.astype(np.float32),
        "wt": (np.random.uniform(0.5, 1.5, (B, R, 1)) * N / np.sqrt(R) * z).astype(np.float32),
        "xm": (x.transpose(0, 2, 1) / z).astype(np.float32),
        "offs": striped(idx),
    }


def reference(xT, wT, y, wt, xm, offs):
    idx = unstriped(offs)
    pick = lambda x: x[:, idx].reshape(x.shape[0], B, N).transpose(1, 0, 2)
    a = mxq(f64(xT), 1, "e4m3").transpose(0, 2, 1) @ mxq(pick(f64(wT)), 1, "e4m3")
    e = np.exp(a - a.max(-1, keepdims=True))
    g = f64(wt) * (e / e.sum(-1, keepdims=True) - f64(y))
    dw = mxq(f64(xm), 1, "e4m3").transpose(0, 2, 1) @ mxq(g, 1, "e5m2")
    gw = np.zeros((D, T))
    gw[:, idx] = dw.transpose(1, 0, 2).reshape(D, B * N)
    return gw

@@ -1,0 +1,209 @@
+from contextlib import ExitStack
+
+import concourse.mybir as mybir
+
+D, T, R, N = 512, 2048, 1024, 512
+P, PACK = 128, 4
+PASSES = R // (P * PACK)
+CHUNKS = D // P
+FLOPS = 2 * 2 * D * R * N
+
+F32 = mybir.dt.float32
+BF16 = mybir.dt.bfloat16
+U32 = mybir.dt.uint32
+U16 = mybir.dt.uint16
+U8 = mybir.dt.uint8
+E4 = mybir.dt.float8_e4m3fn_x4
+E5 = mybir.dt.float8_e5m2_x4
+ALU = mybir.AluOpType
+ACT = mybir.ActivationFunctionType
+AX = mybir.AxisListType
+
+
+def tile_attend_gkl_w_kernel(tc, xT, wT, y, wt, xm, offs, out):
+    nc = tc.nc
+
+    def vcopy(o, i):
+        nc.vector.tensor_copy(out=o, in_=i)
+
+    def scopy(o, i):
+        nc.scalar.copy(out=o, in_=i)
+
+    with ExitStack() as ctx:
+        held = ctx.enter_context(tc.tile_pool(name="held", bufs=1))
+        sb = ctx.enter_context(tc.tile_pool(name="sb", bufs=1))
+        ps_s = ctx.enter_context(tc.psum_pool(name="ps_s", bufs=6))
+        ps_o = ctx.enter_context(tc.psum_pool(name="ps_o", bufs=2))
+
+        offsets = held.tile([P, N // 16], U16, name="offsets")
+        x_raw = [sb.tile([P, PACK, 512], F32, name=f"x_raw{g}") for g in range(PASSES)]
+        w_raw = [sb.tile([P, T], F32, name=f"w_raw{j}") for j in range(PACK)]
+        y_raw = [sb.tile([P, PACK, N], F32, name=f"y_raw{g}") for g in range(PASSES)]
+        m_raw = [sb.tile([P, PACK, D], F32, name=f"m_raw{g}") for g in range(PASSES)]
+        wt_sb = sb.tile([P, PASSES, 8], F32, name="wt_sb")
+        windows = [sb.tile([P, T], F32, name=f"window{c}") for c in range(CHUNKS)]
+
+        x_planes = xT[0].rearrange("(p j) r -> p j r", j=PACK)
+        w_planes = wT.rearrange("(p j) c -> p j c", j=PACK)
+
+        def rows(ap, g):
+            return ap[0, 512 * g : 512 * (g + 1), :].rearrange("(p t) n -> p t n", t=PACK)
+
+        nc.sync.dma_start(out=x_raw[0][:], in_=x_planes[:, :, 0:512])
+        nc.sync.dma_start(offsets[:], offs)
+        for j in range(PACK):
+            nc.sync.dma_start(out=w_raw[j][:], in_=w_planes[:, j, :])
+        nc.sync.dma_start(out=y_raw[0][:], in_=rows(y, 0))
+        nc.sync.dma_start(out=wt_sb[:, :, 0:PACK], in_=wt[0].rearrange("(g p t) o -> p g (t o)", g=PASSES, t=PACK))
+        nc.sync.dma_start(out=x_raw[1][:], in_=x_planes[:, :, 512:1024])
+        nc.sync.dma_start(out=y_raw[1][:], in_=rows(y, 1))
+        for g in range(PASSES):
+            nc.sync.dma_start(out=m_raw[g][:], in_=rows(xm, g))
+
+        warm = sb.tile([P, 2], F32, name="warm")
+        nc.vector.memset(warm[:, 0:1], 0.0)
+        nc.scalar.activation(out=warm[:, 1:2], in_=warm[:, 0:1], func=ACT.Exp)
+
+        for c in range(CHUNKS):
+            nc.vector.memset(windows[c][:], 0.0)
+
+        x_bf = [sb.tile([P, 2048], BF16, name=f"x_bf{g}", align_bytes=64) for g in range(PASSES)]
+        x_codes = [sb.tile([P, 512], U32, name=f"x_codes{g}", align_bytes=64) for g in range(PASSES)]
+        x_scales = [sb.tile([P, 512], U8, name=f"x_scales{g}", align_bytes=64) for g in range(PASSES)]
+
+        def prepare_x(g):
+            scopy(
+                x_bf[g][:].rearrange("p (t m j) -> p m j t", t=PACK, j=PACK),
+                x_raw[g][:].rearrange("p j (m t) -> p m j t", t=PACK),
+            )
+            nc.vector.quantize_mx(out=x_codes[g][:].bitcast(E4), scales=x_scales[g][:], in_=x_bf[g][:])
+
+        prepare_x(0)
+
+        w_bf = sb.tile([P, N, PACK], BF16, name="w_bf", align_bytes=64)
+        w_codes = sb.tile([P, N], U32, name="w_codes", align_bytes=64)
+        w_scales = sb.tile([P, N], U8, name="w_scales", align_bytes=64)
+        for j in range(PACK):
+            vcopy(w_bf[:, :, j], w_raw[j][:].indirect(offsets[:]))
+        nc.vector.quantize_mx(out=w_codes[:].bitcast(E4), scales=w_scales[:], in_=w_bf[:].rearrange("p n j -> p (n j)"))
+
+        neg_max = sb.tile([P, PASSES * PACK], F32, name="neg_max")
+        sums = sb.tile([P, PASSES * PACK], F32, name="sums")
+        inv = sb.tile([P, PASSES * PACK], F32, name="inv")
+        coef = sb.tile([P, PASSES * PACK], F32, name="coef")
+        e_sb = [sb.tile([P, PACK, N], F32, name=f"e_sb{g}") for g in range(PASSES)]
+        yw = [sb.tile([P, PACK, N], F32, name=f"yw{g}") for g in range(PASSES)]
+        g_pl = [sb.tile([P, PACK, N], BF16, name=f"g_pl{g}") for g in range(PASSES)]
+        g_bf = [sb.tile([P, N, PACK], BF16, name=f"g_bf{g}", align_bytes=64) for g in range(PASSES)]
+        g_codes = [sb.tile([P, N], U32, name=f"g_codes{g}", align_bytes=64) for g in range(PASSES)]
+        g_scales = [sb.tile([P, N], U8, name=f"g_scales{g}", align_bytes=64) for g in range(PASSES)]
+
+        def scores(i):
+            g, t = divmod(i, PACK)
+            cols = slice(P * t, P * (t + 1))
+            acc = ps_s.tile([P, N], F32, name="acc")
+            nc.tensor.matmul_mx(
+                out=acc[:],
+                lhsT=x_codes[g][:, cols].bitcast(E4),
+                lhsT_scale=x_scales[g][:, cols],
+                rhs=w_codes[:].bitcast(E4),
+                rhs_scale=w_scales[:],
+                start=True,
+                stop=True,
+            )
+            nc.vector.tensor_reduce(out=neg_max[:, i : i + 1], in_=acc[:], axis=AX.X, op=ALU.max, negate=True)
+            nc.scalar.activation(
+                out=e_sb[g][:, t, :], in_=acc[:], func=ACT.Exp, bias=neg_max[:, i : i + 1], accum_out=sums[:, i : i + 1]
+            )
+
+        def weigh_y(i):
+            g, t = divmod(i, PACK)
+            nc.scalar.activation(out=yw[g][:, t, :], in_=y_raw[g][:, t, :], func=ACT.Copy, scale=wt_sb[:, g, t : t + 1])
+
+        def coefs(i, n):
+            g, t = divmod(i, PACK)
+            nc.vector.reciprocal(out=inv[:, i : i + n], in_=sums[:, i : i + n])
+            nc.vector.tensor_tensor(out=coef[:, i : i + n], in0=inv[:, i : i + n], in1=wt_sb[:, g, t : t + n], op=ALU.mult)
+
+        def grad(i):
+            g, t = divmod(i, PACK)
+            nc.vector.scalar_tensor_tensor(
+                out=g_pl[g][:, t, :], in0=e_sb[g][:, t, :], scalar=coef[:, i : i + 1], in1=yw[g][:, t, :],
+                op0=ALU.mult, op1=ALU.subtract,
+            )
+
+        def interleave(copy, dst, src):
+            copy(dst.rearrange("p (c i) t -> p c t i", i=4), src.rearrange("p t (c i) -> p c t i", i=4))
+
+        def quant_g(g, split):
+            if split > 0:
+                interleave(scopy, g_bf[g][:, 0:split, :], g_pl[g][:, :, 0:split])
+            if split < N:
+                interleave(vcopy, g_bf[g][:, split:N, :], g_pl[g][:, :, split:N])
+            nc.vector.quantize_mx(
+                out=g_codes[g][:].bitcast(E5), scales=g_scales[g][:], in_=g_bf[g][:].rearrange("p n t -> p (n t)")
+            )
+
+        m_bf = [sb.tile([P, PASSES, P, PACK], BF16, name=f"m_bf{c}", align_bytes=64) for c in range(CHUNKS)]
+        m_codes = [sb.tile([P, PASSES * P], U32, name=f"m_codes{c}", align_bytes=64) for c in range(CHUNKS)]
+        m_scales = [sb.tile([P, PASSES * P], U8, name=f"m_scales{c}", align_bytes=64) for c in range(CHUNKS)]
+        res = [sb.tile([P, N], F32, name=f"res{c}") for c in range(CHUNKS)]
+
+        def prepare_m(c):
+            for g in range(PASSES):
+                interleave(scopy, m_bf[c][:, g, :, :], m_raw[g][:, :, P * c : P * (c + 1)])
+            nc.vector.quantize_mx(
+                out=m_codes[c][:].bitcast(E4), scales=m_scales[c][:], in_=m_bf[c][:].rearrange("p g d t -> p (g d t)")
+            )
+
+        scores(0)
+        scores(1)
+        weigh_y(0)
+        weigh_y(1)
+        scores(2)
+        scores(3)
+        prepare_x(1)
+        coefs(0, 2)
+        grad(0)
+        grad(1)
+        weigh_y(2)
+        weigh_y(3)
+        coefs(2, 2)
+        scores(4)
+        scores(5)
+        grad(2)
+        grad(3)
+        weigh_y(4)
+        weigh_y(5)
+        scores(6)
+        scores(7)
+        coefs(4, 2)
+        weigh_y(6)
+        weigh_y(7)
+        grad(4)
+        grad(5)
+        coefs(6, 2)
+        quant_g(0, 0)
+        grad(6)
+        grad(7)
+        prepare_m(0)
+        quant_g(1, 192)
+
+        for c in range(CHUNKS):
+            acc = ps_o.tile([P, N], F32, name="acc_o")
+            for g in range(PASSES):
+                cols = slice(P * g, P * (g + 1))
+                nc.tensor.matmul_mx(
+                    out=acc[:],
+                    lhsT=m_codes[c][:, cols].bitcast(E4),
+                    lhsT_scale=m_scales[c][:, cols],
+                    rhs=g_codes[g][:].bitcast(E5),
+                    rhs_scale=g_scales[g][:],
+                    start=(g == 0),
+                    stop=(g == PASSES - 1),
+                )
+            scopy(res[c][:], acc[:])
+            if c + 1 < CHUNKS:
+                prepare_m(c + 1)
+            vcopy(windows[c][:].indirect(offsets[:]), res[c][:])
+            nc.sync.dma_start(out=out[P * c : P * (c + 1), :], in_=windows[c][:])

@@ -36,12 +36,13 @@ def tile_attend_gkl_w_kernel(tc, xT, wT, y, wt, xm, offs, out):
         ps_o = ctx.enter_context(tc.psum_pool(name="ps_o", bufs=2))
 
         offsets = held.tile([P, N // 16], U16, name="offsets")
-        x_raw = [sb.tile([P, PACK, 512], F32, name=f"x_raw{g}") for g in range(PASSES)]
+        x1_raw = sb.tile([P, PACK, 512], F32, name="x1_raw")
         w_raw = [sb.tile([P, T], F32, name=f"w_raw{j}") for j in range(PACK)]
         y_raw = [sb.tile([P, PACK, N], F32, name=f"y_raw{g}") for g in range(PASSES)]
         m_raw = [sb.tile([P, PACK, D], F32, name=f"m_raw{g}") for g in range(PASSES)]
         wt_sb = sb.tile([P, PASSES, 8], F32, name="wt_sb")
-        windows = [sb.tile([P, T], F32, name=f"window{c}") for c in range(CHUNKS)]
+        windows = [sb.tile([P, T], F32, name=f"window{c}") for c in range(3)]
+        x0_half = [sb.tile([P, PACK, 256], F32, name=f"x0_half{h}") for h in range(2)]
 
         x_planes = xT[0].rearrange("(p j) r -> p j r", j=PACK)
         w_planes = wT.rearrange("(p j) c -> p j c", j=PACK)
@@ -49,13 +50,14 @@ def tile_attend_gkl_w_kernel(tc, xT, wT, y, wt, xm, offs, out):
         def rows(ap, g):
             return ap[0, 512 * g : 512 * (g + 1), :].rearrange("(p t) n -> p t n", t=PACK)
 
-        nc.sync.dma_start(out=x_raw[0][:], in_=x_planes[:, :, 0:512])
         nc.sync.dma_start(offsets[:], offs)
         for j in range(PACK):
             nc.sync.dma_start(out=w_raw[j][:], in_=w_planes[:, j, :])
+        nc.scalar.dma_start(out=wt_sb[:, :, 0:PACK], in_=wt[0].rearrange("(g p t) o -> p g (t o)", g=PASSES, t=PACK))
+        for h in range(2):
+            nc.sync.dma_start(out=x0_half[h][:], in_=x_planes[:, :, 256 * h : 256 * (h + 1)])
         nc.sync.dma_start(out=y_raw[0][:], in_=rows(y, 0))
-        nc.sync.dma_start(out=wt_sb[:, :, 0:PACK], in_=wt[0].rearrange("(g p t) o -> p g (t o)", g=PASSES, t=PACK))
-        nc.sync.dma_start(out=x_raw[1][:], in_=x_planes[:, :, 512:1024])
+        nc.sync.dma_start(out=x1_raw[:], in_=x_planes[:, :, 512:1024])
         nc.sync.dma_start(out=y_raw[1][:], in_=rows(y, 1))
         for g in range(PASSES):
             nc.sync.dma_start(out=m_raw[g][:], in_=rows(xm, g))
@@ -64,28 +66,36 @@ def tile_attend_gkl_w_kernel(tc, xT, wT, y, wt, xm, offs, out):
         nc.vector.memset(warm[:, 0:1], 0.0)
         nc.scalar.activation(out=warm[:, 1:2], in_=warm[:, 0:1], func=ACT.Exp)
 
-        for c in range(CHUNKS):
-            nc.vector.memset(windows[c][:], 0.0)
+        for win in windows:
+            nc.vector.memset(win[:], 0.0)
 
         x_bf = [sb.tile([P, 2048], BF16, name=f"x_bf{g}", align_bytes=64) for g in range(PASSES)]
         x_codes = [sb.tile([P, 512], U32, name=f"x_codes{g}", align_bytes=64) for g in range(PASSES)]
         x_scales = [sb.tile([P, 512], U8, name=f"x_scales{g}", align_bytes=64) for g in range(PASSES)]
 
-        def prepare_x(g):
-            scopy(
-                x_bf[g][:].rearrange("p (t m j) -> p m j t", t=PACK, j=PACK),
-                x_raw[g][:].rearrange("p j (m t) -> p m j t", t=PACK),
+        def cast_x(copy, g, raw, m0, m1):
+            copy(
+                x_bf[g][:].rearrange("p (t m j) -> p m j t", t=PACK, j=PACK)[:, m0:m1, :, :],
+                raw[:].rearrange("p j (m t) -> p m j t", t=PACK),
             )
-            nc.vector.quantize_mx(out=x_codes[g][:].bitcast(E4), scales=x_scales[g][:], in_=x_bf[g][:])
 
-        prepare_x(0)
+        def quant_x(g, t0, t1):
+            nc.vector.quantize_mx(
+                out=x_codes[g][:, P * t0 : P * t1].bitcast(E4),
+                scales=x_scales[g][:, P * t0 : P * t1],
+                in_=x_bf[g][:, 512 * t0 : 512 * t1],
+            )
 
         w_bf = sb.tile([P, N, PACK], BF16, name="w_bf", align_bytes=64)
         w_codes = sb.tile([P, N], U32, name="w_codes", align_bytes=64)
         w_scales = sb.tile([P, N], U8, name="w_scales", align_bytes=64)
         for j in range(PACK):
             vcopy(w_bf[:, :, j], w_raw[j][:].indirect(offsets[:]))
+        cast_x(scopy, 0, x0_half[0], 0, 64)
         nc.vector.quantize_mx(out=w_codes[:].bitcast(E4), scales=w_scales[:], in_=w_bf[:].rearrange("p n j -> p (n j)"))
+        cast_x(vcopy, 0, x0_half[1], 64, 128)
+        quant_x(0, 0, 2)
+        quant_x(0, 2, 4)
 
         neg_max = sb.tile([P, PASSES * PACK], F32, name="neg_max")
         sums = sb.tile([P, PASSES * PACK], F32, name="sums")
@@ -120,9 +130,11 @@ def tile_attend_gkl_w_kernel(tc, xT, wT, y, wt, xm, offs, out):
             g, t = divmod(i, PACK)
             nc.scalar.activation(out=yw[g][:, t, :], in_=y_raw[g][:, t, :], func=ACT.Copy, scale=wt_sb[:, g, t : t + 1])
 
+        def recip(i, n):
+            nc.vector.reciprocal(out=inv[:, i : i + n], in_=sums[:, i : i + n])
+
         def coefs(i, n):
             g, t = divmod(i, PACK)
-            nc.vector.reciprocal(out=inv[:, i : i + n], in_=sums[:, i : i + n])
             nc.vector.tensor_tensor(out=coef[:, i : i + n], in0=inv[:, i : i + n], in1=wt_sb[:, g, t : t + n], op=ALU.mult)
 
         def grad(i):
@@ -135,11 +147,10 @@ def tile_attend_gkl_w_kernel(tc, xT, wT, y, wt, xm, offs, out):
         def interleave(copy, dst, src):
             copy(dst.rearrange("p (c i) t -> p c t i", i=4), src.rearrange("p t (c i) -> p c t i", i=4))
 
-        def quant_g(g, split):
-            if split > 0:
-                interleave(scopy, g_bf[g][:, 0:split, :], g_pl[g][:, :, 0:split])
-            if split < N:
-                interleave(vcopy, g_bf[g][:, split:N, :], g_pl[g][:, :, split:N])
+        def weave_g(copy, g, n0, n1):
+            interleave(copy, g_bf[g][:, n0:n1, :], g_pl[g][:, :, n0:n1])
+
+        def quant_g(g):
             nc.vector.quantize_mx(
                 out=g_codes[g][:].bitcast(E5), scales=g_scales[g][:], in_=g_bf[g][:].rearrange("p n t -> p (n t)")
             )
@@ -149,47 +160,16 @@ def tile_attend_gkl_w_kernel(tc, xT, wT, y, wt, xm, offs, out):
         m_scales = [sb.tile([P, PASSES * P], U8, name=f"m_scales{c}", align_bytes=64) for c in range(CHUNKS)]
         res = [sb.tile([P, N], F32, name=f"res{c}") for c in range(CHUNKS)]
 
-        def prepare_m(c):
+        def cast_m(copy, c):
             for g in range(PASSES):
-                interleave(scopy, m_bf[c][:, g, :, :], m_raw[g][:, :, P * c : P * (c + 1)])
+                interleave(copy, m_bf[c][:, g, :, :], m_raw[g][:, :, P * c : P * (c + 1)])
+
+        def quant_m(c):
             nc.vector.quantize_mx(
                 out=m_codes[c][:].bitcast(E4), scales=m_scales[c][:], in_=m_bf[c][:].rearrange("p g d t -> p (g d t)")
             )
 
-        scores(0)
-        scores(1)
-        weigh_y(0)
-        weigh_y(1)
-        scores(2)
-        scores(3)
-        prepare_x(1)
-        coefs(0, 2)
-        grad(0)
-        grad(1)
-        weigh_y(2)
-        weigh_y(3)
-        coefs(2, 2)
-        scores(4)
-        scores(5)
-        grad(2)
-        grad(3)
-        weigh_y(4)
-        weigh_y(5)
-        scores(6)
-        scores(7)
-        coefs(4, 2)
-        weigh_y(6)
-        weigh_y(7)
-        grad(4)
-        grad(5)
-        coefs(6, 2)
-        quant_g(0, 0)
-        grad(6)
-        grad(7)
-        prepare_m(0)
-        quant_g(1, 192)
-
-        for c in range(CHUNKS):
+        def product(c):
             acc = ps_o.tile([P, N], F32, name="acc_o")
             for g in range(PASSES):
                 cols = slice(P * g, P * (g + 1))
@@ -203,7 +183,65 @@ def tile_attend_gkl_w_kernel(tc, xT, wT, y, wt, xm, offs, out):
                     stop=(g == PASSES - 1),
                 )
             scopy(res[c][:], acc[:])
-            if c + 1 < CHUNKS:
-                prepare_m(c + 1)
-            vcopy(windows[c][:].indirect(offsets[:]), res[c][:])
-            nc.sync.dma_start(out=out[P * c : P * (c + 1), :], in_=windows[c][:])
+
+        def scatter(c):
+            win = windows[c % 3]
+            vcopy(win[:].indirect(offsets[:]), res[c][:])
+            nc.sync.dma_start(out=out[P * c : P * (c + 1), :], in_=win[:])
+
+        scores(0)
+        scores(1)
+        weigh_y(0)
+        weigh_y(1)
+        scores(2)
+        scores(3)
+        weigh_y(2)
+        weigh_y(3)
+        recip(0, 2)
+        cast_x(vcopy, 1, x1_raw, 0, 128)
+        coefs(0, 2)
+        quant_x(1, 0, 4)
+        recip(2, 2)
+        grad(0)
+        coefs(2, 2)
+        grad(1)
+        scores(4)
+        weigh_y(4)
+        weigh_y(5)
+        grad(2)
+        scores(5)
+        grad(3)
+        scores(6)
+        weigh_y(6)
+        recip(4, 2)
+        scores(7)
+        weigh_y(7)
+        coefs(4, 2)
+        grad(4)
+        grad(5)
+        recip(6, 2)
+        weave_g(vcopy, 0, 0, 128)
+        coefs(6, 2)
+        cast_m(scopy, 0)
+        quant_m(0)
+        grad(6)
+        grad(7)
+        weave_g(scopy, 0, 128, 512)
+        weave_g(vcopy, 1, 0, 384)
+        weave_g(scopy, 1, 384, 512)
+        quant_g(0)
+        quant_g(1)
+        product(0)
+        cast_m(vcopy, 1)
+        quant_m(1)
+        product(1)
+        scatter(0)
+        cast_m(scopy, 2)
+        quant_m(2)
+        product(2)
+        scatter(1)
+        cast_m(scopy, 3)
+        quant_m(3)
+        product(3)
+        scatter(2)
+        scatter(3)

@@ -56,8 +56,9 @@ def tile_attend_gkl_w_kernel(tc, xT, wT, y, wt, xm, offs, out):
         nc.scalar.dma_start(out=wt_sb[:, :, 0:PACK], in_=wt[0].rearrange("(g p t) o -> p g (t o)", g=PASSES, t=PACK))
         for h in range(2):
             nc.sync.dma_start(out=x0_half[h][:], in_=x_planes[:, :, 256 * h : 256 * (h + 1)])
-        nc.sync.dma_start(out=y_raw[0][:], in_=rows(y, 0))
+        nc.sync.dma_start(out=y_raw[0][:, 0:2, :], in_=rows(y, 0)[:, 0:2, :])
         nc.sync.dma_start(out=x1_raw[:], in_=x_planes[:, :, 512:1024])
+        nc.sync.dma_start(out=y_raw[0][:, 2:4, :], in_=rows(y, 0)[:, 2:4, :])
         nc.sync.dma_start(out=y_raw[1][:], in_=rows(y, 1))
         for g in range(PASSES):
             nc.sync.dma_start(out=m_raw[g][:], in_=rows(xm, g))
@@ -75,8 +76,8 @@ def tile_attend_gkl_w_kernel(tc, xT, wT, y, wt, xm, offs, out):
 
         def cast_x(copy, g, raw, m0, m1):
             copy(
-                x_bf[g][:].rearrange("p (t m j) -> p m j t", t=PACK, j=PACK)[:, m0:m1, :, :],
-                raw[:].rearrange("p j (m t) -> p m j t", t=PACK),
+                x_bf[g][:].rearrange("p (t m j) -> p m t j", t=PACK, j=PACK)[:, m0:m1, :, :],
+                raw[:].rearrange("p j (m t) -> p m t j", t=PACK),
             )
 
         def quant_x(g, t0, t1):
@@ -94,7 +95,8 @@ def tile_attend_gkl_w_kernel(tc, xT, wT, y, wt, xm, offs, out):
         cast_x(scopy, 0, x0_half[0], 0, 64)
         nc.vector.quantize_mx(out=w_codes[:].bitcast(E4), scales=w_scales[:], in_=w_bf[:].rearrange("p n j -> p (n j)"))
         cast_x(vcopy, 0, x0_half[1], 64, 128)
-        quant_x(0, 0, 2)
+        quant_x(0, 0, 1)
+        quant_x(0, 1, 2)
         quant_x(0, 2, 4)
 
         neg_max = sb.tile([P, PASSES * PACK], F32, name="neg_max")
@@ -103,7 +105,10 @@ def tile_attend_gkl_w_kernel(tc, xT, wT, y, wt, xm, offs, out):
         coef = sb.tile([P, PASSES * PACK], F32, name="coef")
         e_sb = [sb.tile([P, PACK, N], F32, name=f"e_sb{g}") for g in range(PASSES)]
         yw = [sb.tile([P, PACK, N], F32, name=f"yw{g}") for g in range(PASSES)]
-        g_pl = [sb.tile([P, PACK, N], BF16, name=f"g_pl{g}") for g in range(PASSES)]
+        g_pl = [
+            sb.tile([P, PACK, N], BF16, name="g_pl0"),
+            sb.tile([P, PACK, N], BF16, name="g_pl1", tag="late", align_bytes=64),
+        ]
         g_bf = [sb.tile([P, N, PACK], BF16, name=f"g_bf{g}", align_bytes=64) for g in range(PASSES)]
         g_codes = [sb.tile([P, N], U32, name=f"g_codes{g}", align_bytes=64) for g in range(PASSES)]
         g_scales = [sb.tile([P, N], U8, name=f"g_scales{g}", align_bytes=64) for g in range(PASSES)]
@@ -155,28 +160,37 @@ def tile_attend_gkl_w_kernel(tc, xT, wT, y, wt, xm, offs, out):
                 out=g_codes[g][:].bitcast(E5), scales=g_scales[g][:], in_=g_bf[g][:].rearrange("p n t -> p (n t)")
             )
 
-        m_bf = [sb.tile([P, PASSES, P, PACK], BF16, name=f"m_bf{c}", align_bytes=64) for c in range(CHUNKS)]
-        m_codes = [sb.tile([P, PASSES * P], U32, name=f"m_codes{c}", align_bytes=64) for c in range(CHUNKS)]
-        m_scales = [sb.tile([P, PASSES * P], U8, name=f"m_scales{c}", align_bytes=64) for c in range(CHUNKS)]
+        m_bf = {}
+        m_codes = sb.tile([P, CHUNKS * PASSES * P], U32, name="m_codes", align_bytes=64)
+        m_scales = sb.tile([P, CHUNKS * PASSES * P], U8, name="m_scales", align_bytes=64)
         res = [sb.tile([P, N], F32, name=f"res{c}") for c in range(CHUNKS)]
 
-        def cast_m(copy, c):
-            for g in range(PASSES):
-                interleave(copy, m_bf[c][:, g, :, :], m_raw[g][:, :, P * c : P * (c + 1)])
+        def stage_m(c0, c1, tag):
+            tile = sb.tile([P, c1 - c0, PASSES, P, PACK], BF16, name=f"m_bf{c0}", tag=tag, align_bytes=64)
+            for c in range(c0, c1):
+                m_bf[c] = (tile, c - c0)
 
-        def quant_m(c):
+        def cast_m(copy, c):
+            tile, k = m_bf[c]
+            for g in range(PASSES):
+                interleave(copy, tile[:, k, g, :, :], m_raw[g][:, :, P * c : P * (c + 1)])
+
+        def quant_m(c0, c1):
+            cols = slice(PASSES * P * c0, PASSES * P * c1)
             nc.vector.quantize_mx(
-                out=m_codes[c][:].bitcast(E4), scales=m_scales[c][:], in_=m_bf[c][:].rearrange("p g d t -> p (g d t)")
+                out=m_codes[:, cols].bitcast(E4),
+                scales=m_scales[:, cols],
+                in_=m_bf[c0][0][:].rearrange("p c g d t -> p (c g d t)"),
             )
 
         def product(c):
             acc = ps_o.tile([P, N], F32, name="acc_o")
             for g in range(PASSES):
-                cols = slice(P * g, P * (g + 1))
+                cols = slice(P * (PASSES * c + g), P * (PASSES * c + g + 1))
                 nc.tensor.matmul_mx(
                     out=acc[:],
-                    lhsT=m_codes[c][:, cols].bitcast(E4),
-                    lhsT_scale=m_scales[c][:, cols],
+                    lhsT=m_codes[:, cols].bitcast(E4),
+                    lhsT_scale=m_scales[:, cols],
                     rhs=g_codes[g][:].bitcast(E5),
                     rhs_scale=g_scales[g][:],
                     start=(g == 0),
@@ -189,59 +203,61 @@ def tile_attend_gkl_w_kernel(tc, xT, wT, y, wt, xm, offs, out):
             vcopy(win[:].indirect(offsets[:]), res[c][:])
             nc.sync.dma_start(out=out[P * c : P * (c + 1), :], in_=win[:])
 
-        scores(0)
-        scores(1)
         weigh_y(0)
         weigh_y(1)
+        scores(0)
+        scores(1)
+        cast_x(vcopy, 1, x1_raw, 0, 128)
         scores(2)
+        recip(0, 2)
         scores(3)
         weigh_y(2)
         weigh_y(3)
-        recip(0, 2)
-        cast_x(vcopy, 1, x1_raw, 0, 128)
         coefs(0, 2)
         quant_x(1, 0, 4)
-        recip(2, 2)
         grad(0)
-        coefs(2, 2)
+        recip(2, 2)
         grad(1)
         scores(4)
+        scores(5)
+        scores(6)
+        coefs(2, 2)
+        scores(7)
         weigh_y(4)
         weigh_y(5)
-        grad(2)
-        scores(5)
-        grad(3)
-        scores(6)
         weigh_y(6)
-        recip(4, 2)
-        scores(7)
         weigh_y(7)
+        grad(2)
+        recip(4, 2)
+        grad(3)
         coefs(4, 2)
-        grad(4)
-        grad(5)
-        recip(6, 2)
         weave_g(vcopy, 0, 0, 128)
-        coefs(6, 2)
+        recip(6, 2)
+        weave_g(scopy, 0, 128, 512)
+        stage_m(0, 1, "early")
         cast_m(scopy, 0)
-        quant_m(0)
+        grad(4)
+        coefs(6, 2)
+        grad(5)
         grad(6)
         grad(7)
-        weave_g(scopy, 0, 128, 512)
-        weave_g(vcopy, 1, 0, 384)
-        weave_g(scopy, 1, 384, 512)
         quant_g(0)
+        weave_g(vcopy, 1, 0, 320)
+        weave_g(scopy, 1, 320, 512)
+        quant_m(0, 1)
         quant_g(1)
         product(0)
-        cast_m(vcopy, 1)
-        quant_m(1)
+        stage_m(1, 3, "late")
+        cast_m(scopy, 1)
+        cast_m(vcopy, 2)
+        quant_m(1, 3)
         product(1)
         scatter(0)
-        cast_m(scopy, 2)
-        quant_m(2)
+        stage_m(3, 4, "late")
+        cast_m(scopy, 3)
+        quant_m(3, 4)
         product(2)
         scatter(1)
-        cast_m(scopy, 3)
-        quant_m(3)
         product(3)
         scatter(2)
         scatter(3)

@@ -50,12 +50,13 @@ def tile_attend_gkl_w_kernel(tc, xT, wT, y, wt, xm, offs, out):
         def rows(ap, g):
             return ap[0, 512 * g : 512 * (g + 1), :].rearrange("(p t) n -> p t n", t=PACK)
 
+        nc.sync.dma_start(out=w_raw[0][:], in_=w_planes[:, 0, :])
         nc.sync.dma_start(offsets[:], offs)
-        for j in range(PACK):
+        for j in range(1, PACK):
             nc.sync.dma_start(out=w_raw[j][:], in_=w_planes[:, j, :])
-        nc.scalar.dma_start(out=wt_sb[:, :, 0:PACK], in_=wt[0].rearrange("(g p t) o -> p g (t o)", g=PASSES, t=PACK))
         for h in range(2):
             nc.sync.dma_start(out=x0_half[h][:], in_=x_planes[:, :, 256 * h : 256 * (h + 1)])
+        nc.sync.dma_start(out=wt_sb[:, :, 0:PACK], in_=wt[0].rearrange("(g p t) o -> p g (t o)", g=PASSES, t=PACK))
         nc.sync.dma_start(out=y_raw[0][:, 0:2, :], in_=rows(y, 0)[:, 0:2, :])
         nc.sync.dma_start(out=x1_raw[:], in_=x_planes[:, :, 512:1024])
         nc.sync.dma_start(out=y_raw[0][:, 2:4, :], in_=rows(y, 0)[:, 2:4, :])
@@ -196,19 +197,28 @@ def tile_attend_gkl_w_kernel(tc, xT, wT, y, wt, xm, offs, out):
                     start=(g == 0),
                     stop=(g == PASSES - 1),
                 )
-            scopy(res[c][:], acc[:])
+            for n0, n1 in pieces(c):
+                scopy(res[c][:, n0:n1], acc[:, n0:n1])
+
+        def pieces(c):
+            return [(0, N // 2), (N // 2, N)] if c == 0 else [(0, N)]
 
         def scatter(c):
             win = windows[c % 3]
-            vcopy(win[:].indirect(offsets[:]), res[c][:])
-            nc.sync.dma_start(out=out[P * c : P * (c + 1), :], in_=win[:])
+            for n0, n1 in pieces(c):
+                vcopy(win[:].indirect(offsets[:, n0 // 16 : n1 // 16]), res[c][:, n0:n1])
+            if c + 1 < CHUNKS:
+                nc.sync.dma_start(out=out[P * c : P * (c + 1), :], in_=win[:])
+            else:
+                nc.sync.dma_start(out=out[P * c : P * (c + 1), 0 : T // 2], in_=win[:, 0 : T // 2])
+                nc.scalar.dma_start(out=out[P * c : P * (c + 1), T // 2 : T], in_=win[:, T // 2 : T])
 
         weigh_y(0)
         weigh_y(1)
         scores(0)
         scores(1)
-        cast_x(vcopy, 1, x1_raw, 0, 128)
         scores(2)
+        cast_x(vcopy, 1, x1_raw, 0, 128)
         recip(0, 2)
         scores(3)
         weigh_y(2)

@@ -6,6 +6,7 @@ D, T, R, N = 512, 2048, 1024, 512
 P, PACK = 128, 4
 PASSES = R // (P * PACK)
 CHUNKS = D // P
+PAD = N // 2
 FLOPS = 2 * 2 * D * R * N
 
 F32 = mybir.dt.float32
@@ -32,17 +33,16 @@ def tile_attend_gkl_w_kernel(tc, xT, wT, y, wt, xm, offs, out):
     with ExitStack() as ctx:
         held = ctx.enter_context(tc.tile_pool(name="held", bufs=1))
         sb = ctx.enter_context(tc.tile_pool(name="sb", bufs=1))
-        ps_s = ctx.enter_context(tc.psum_pool(name="ps_s", bufs=6))
-        ps_o = ctx.enter_context(tc.psum_pool(name="ps_o", bufs=2))
+        ps_s = ctx.enter_context(tc.psum_pool(name="ps_s", bufs=4))
+        ps_o = ctx.enter_context(tc.psum_pool(name="ps_o", bufs=4))
 
         offsets = held.tile([P, N // 16], U16, name="offsets")
-        x1_raw = sb.tile([P, PACK, 512], F32, name="x1_raw")
+        x_raw = [sb.tile([P, PACK, 512], F32, name=f"x_raw{g}") for g in range(PASSES)]
         w_raw = [sb.tile([P, T], F32, name=f"w_raw{j}") for j in range(PACK)]
         y_raw = [sb.tile([P, PACK, N], F32, name=f"y_raw{g}") for g in range(PASSES)]
         m_raw = [sb.tile([P, PACK, D], F32, name=f"m_raw{g}") for g in range(PASSES)]
         wt_sb = sb.tile([P, PASSES, 8], F32, name="wt_sb")
         windows = [sb.tile([P, T], F32, name=f"window{c}") for c in range(3)]
-        x0_half = [sb.tile([P, PACK, 256], F32, name=f"x0_half{h}") for h in range(2)]
 
         x_planes = xT[0].rearrange("(p j) r -> p j r", j=PACK)
         w_planes = wT.rearrange("(p j) c -> p j c", j=PACK)
@@ -54,31 +54,27 @@ def tile_attend_gkl_w_kernel(tc, xT, wT, y, wt, xm, offs, out):
         nc.sync.dma_start(offsets[:], offs)
         for j in range(1, PACK):
             nc.sync.dma_start(out=w_raw[j][:], in_=w_planes[:, j, :])
-        for h in range(2):
-            nc.sync.dma_start(out=x0_half[h][:], in_=x_planes[:, :, 256 * h : 256 * (h + 1)])
+        nc.sync.dma_start(out=x_raw[0][:], in_=x_planes[:, :, 0:512])
         nc.sync.dma_start(out=wt_sb[:, :, 0:PACK], in_=wt[0].rearrange("(g p t) o -> p g (t o)", g=PASSES, t=PACK))
         nc.sync.dma_start(out=y_raw[0][:, 0:2, :], in_=rows(y, 0)[:, 0:2, :])
-        nc.sync.dma_start(out=x1_raw[:], in_=x_planes[:, :, 512:1024])
         nc.sync.dma_start(out=y_raw[0][:, 2:4, :], in_=rows(y, 0)[:, 2:4, :])
+        nc.sync.dma_start(out=x_raw[1][:], in_=x_planes[:, :, 512:1024])
         nc.sync.dma_start(out=y_raw[1][:], in_=rows(y, 1))
         for g in range(PASSES):
             nc.sync.dma_start(out=m_raw[g][:], in_=rows(xm, g))
 
-        warm = sb.tile([P, 2], F32, name="warm")
-        nc.vector.memset(warm[:, 0:1], 0.0)
-        nc.scalar.activation(out=warm[:, 1:2], in_=warm[:, 0:1], func=ACT.Exp)
-
-        for win in windows:
-            nc.vector.memset(win[:], 0.0)
+        nc.vector.memset(windows[0][:], 0.0)
+        nc.vector.memset(windows[1][:], 0.0)
+        nc.gpsimd.memset(windows[2][:], 0.0)
 
         x_bf = [sb.tile([P, 2048], BF16, name=f"x_bf{g}", align_bytes=64) for g in range(PASSES)]
         x_codes = [sb.tile([P, 512], U32, name=f"x_codes{g}", align_bytes=64) for g in range(PASSES)]
         x_scales = [sb.tile([P, 512], U8, name=f"x_scales{g}", align_bytes=64) for g in range(PASSES)]
 
-        def cast_x(copy, g, raw, m0, m1):
+        def cast_x(copy, g, t0, t1):
             copy(
-                x_bf[g][:].rearrange("p (t m j) -> p m t j", t=PACK, j=PACK)[:, m0:m1, :, :],
-                raw[:].rearrange("p j (m t) -> p m t j", t=PACK),
+                x_bf[g][:].rearrange("p (t m j) -> p m j t", t=PACK, j=PACK)[:, :, :, t0:t1],
+                x_raw[g][:].rearrange("p j (m t) -> p m j t", t=PACK)[:, :, :, t0:t1],
             )
 
         def quant_x(g, t0, t1):
@@ -93,9 +89,9 @@ def tile_attend_gkl_w_kernel(tc, xT, wT, y, wt, xm, offs, out):
         w_scales = sb.tile([P, N], U8, name="w_scales", align_bytes=64)
         for j in range(PACK):
             vcopy(w_bf[:, :, j], w_raw[j][:].indirect(offsets[:]))
-        cast_x(scopy, 0, x0_half[0], 0, 64)
         nc.vector.quantize_mx(out=w_codes[:].bitcast(E4), scales=w_scales[:], in_=w_bf[:].rearrange("p n j -> p (n j)"))
-        cast_x(vcopy, 0, x0_half[1], 64, 128)
+        cast_x(vcopy, 0, 0, 2)
+        cast_x(scopy, 0, 2, 4)
         quant_x(0, 0, 1)
         quant_x(0, 1, 2)
         quant_x(0, 2, 4)
@@ -106,13 +102,22 @@ def tile_attend_gkl_w_kernel(tc, xT, wT, y, wt, xm, offs, out):
         coef = sb.tile([P, PASSES * PACK], F32, name="coef")
         e_sb = [sb.tile([P, PACK, N], F32, name=f"e_sb{g}") for g in range(PASSES)]
         yw = [sb.tile([P, PACK, N], F32, name=f"yw{g}") for g in range(PASSES)]
-        g_pl = [
-            sb.tile([P, PACK, N], BF16, name="g_pl0"),
-            sb.tile([P, PACK, N], BF16, name="g_pl1", tag="late", align_bytes=64),
-        ]
+        g_pl0 = sb.tile([P, PACK, N], BF16, name="g_pl0")
+        g_pl1 = [sb.tile([P, PACK, N // 2], BF16, name=f"g_pl1_{h}") for h in range(2)]
+
+        def planes(g, n0, n1):
+            if g == 0:
+                return g_pl0[:, :, n0:n1]
+            h = n0 // (N // 2)
+            return g_pl1[h][:, :, n0 - h * (N // 2) : n1 - h * (N // 2)]
+
         g_bf = [sb.tile([P, N, PACK], BF16, name=f"g_bf{g}", align_bytes=64) for g in range(PASSES)]
-        g_codes = [sb.tile([P, N], U32, name=f"g_codes{g}", align_bytes=64) for g in range(PASSES)]
-        g_scales = [sb.tile([P, N], U8, name=f"g_scales{g}", align_bytes=64) for g in range(PASSES)]
+        g_codes = [sb.tile([P, PAD + N], U32, name=f"g_codes{g}", align_bytes=64) for g in range(PASSES)]
+        g_scales = [sb.tile([P, PAD + N], U8, name=f"g_scales{g}", align_bytes=64) for g in range(PASSES)]
+
+        for g in range(PASSES):
+            nc.vector.memset(g_codes[g][:, 0:PAD], 0)
+            nc.vector.memset(g_scales[g][:, 0:PAD], 0)
 
         def scores(i):
             g, t = divmod(i, PACK)
@@ -136,6 +141,19 @@ def tile_attend_gkl_w_kernel(tc, xT, wT, y, wt, xm, offs, out):
             g, t = divmod(i, PACK)
             nc.scalar.activation(out=yw[g][:, t, :], in_=y_raw[g][:, t, :], func=ACT.Copy, scale=wt_sb[:, g, t : t + 1])
 
+        def weigh_y_vec(i):
+            g, t = divmod(i, PACK)
+            nc.vector.tensor_scalar(
+                out=yw[g][:, t, :], in0=y_raw[g][:, t, :], scalar1=wt_sb[:, g, t : t + 1], scalar2=None, op0=ALU.mult
+            )
+
+        def weigh_y_pool(i):
+            g, t = divmod(i, PACK)
+            nc.gpsimd.tensor_scalar(
+                out=yw[g][:, t, :], in0=y_raw[g][:, t, :], scalar1=wt_sb[:, g, t : t + 1], scalar2=0.0,
+                op0=ALU.mult, op1=ALU.add,
+            )
+
         def recip(i, n):
             nc.vector.reciprocal(out=inv[:, i : i + n], in_=sums[:, i : i + n])
 
@@ -143,10 +161,10 @@ def tile_attend_gkl_w_kernel(tc, xT, wT, y, wt, xm, offs, out):
             g, t = divmod(i, PACK)
             nc.vector.tensor_tensor(out=coef[:, i : i + n], in0=inv[:, i : i + n], in1=wt_sb[:, g, t : t + n], op=ALU.mult)
 
-        def grad(i):
+        def grad(i, n0=0, n1=N):
             g, t = divmod(i, PACK)
             nc.vector.scalar_tensor_tensor(
-                out=g_pl[g][:, t, :], in0=e_sb[g][:, t, :], scalar=coef[:, i : i + 1], in1=yw[g][:, t, :],
+                out=planes(g, n0, n1)[:, t, :], in0=e_sb[g][:, t, n0:n1], scalar=coef[:, i : i + 1], in1=yw[g][:, t, n0:n1],
                 op0=ALU.mult, op1=ALU.subtract,
             )
 
@@ -154,37 +172,33 @@ def tile_attend_gkl_w_kernel(tc, xT, wT, y, wt, xm, offs, out):
             copy(dst.rearrange("p (c i) t -> p c t i", i=4), src.rearrange("p t (c i) -> p c t i", i=4))
 
         def weave_g(copy, g, n0, n1):
-            interleave(copy, g_bf[g][:, n0:n1, :], g_pl[g][:, :, n0:n1])
+            interleave(copy, g_bf[g][:, n0:n1, :], planes(g, n0, n1))
 
-        def quant_g(g):
+        def quant_g(g, n0, n1):
             nc.vector.quantize_mx(
-                out=g_codes[g][:].bitcast(E5), scales=g_scales[g][:], in_=g_bf[g][:].rearrange("p n t -> p (n t)")
+                out=g_codes[g][:, PAD + n0 : PAD + n1].bitcast(E5),
+                scales=g_scales[g][:, PAD + n0 : PAD + n1],
+                in_=g_bf[g][:, n0:n1, :].rearrange("p n t -> p (n t)"),
             )
 
-        m_bf = {}
+        m_bf = [sb.tile([P, PASSES, P, PACK], BF16, name=f"m_bf{c}", tag="m_bf", bufs=2, align_bytes=64) for c in range(CHUNKS)]
         m_codes = sb.tile([P, CHUNKS * PASSES * P], U32, name="m_codes", align_bytes=64)
         m_scales = sb.tile([P, CHUNKS * PASSES * P], U8, name="m_scales", align_bytes=64)
         res = [sb.tile([P, N], F32, name=f"res{c}") for c in range(CHUNKS)]
 
-        def stage_m(c0, c1, tag):
-            tile = sb.tile([P, c1 - c0, PASSES, P, PACK], BF16, name=f"m_bf{c0}", tag=tag, align_bytes=64)
-            for c in range(c0, c1):
-                m_bf[c] = (tile, c - c0)
+        def cast_m(copy, c, passes=range(PASSES)):
+            for g in passes:
+                interleave(copy, m_bf[c][:, g, :, :], m_raw[g][:, :, P * c : P * (c + 1)])
 
-        def cast_m(copy, c):
-            tile, k = m_bf[c]
-            for g in range(PASSES):
-                interleave(copy, tile[:, k, g, :, :], m_raw[g][:, :, P * c : P * (c + 1)])
-
-        def quant_m(c0, c1):
-            cols = slice(PASSES * P * c0, PASSES * P * c1)
+        def quant_m(c):
+            cols = slice(PASSES * P * c, PASSES * P * (c + 1))
             nc.vector.quantize_mx(
                 out=m_codes[:, cols].bitcast(E4),
                 scales=m_scales[:, cols],
-                in_=m_bf[c0][0][:].rearrange("p c g d t -> p (c g d t)"),
+                in_=m_bf[c][:].rearrange("p g d t -> p (g d t)"),
             )
 
-        def product(c):
+        def product(c, first=PAD):
             acc = ps_o.tile([P, N], F32, name="acc_o")
             for g in range(PASSES):
                 cols = slice(P * (PASSES * c + g), P * (PASSES * c + g + 1))
@@ -192,82 +206,87 @@ def tile_attend_gkl_w_kernel(tc, xT, wT, y, wt, xm, offs, out):
                     out=acc[:],
                     lhsT=m_codes[:, cols].bitcast(E4),
                     lhsT_scale=m_scales[:, cols],
-                    rhs=g_codes[g][:].bitcast(E5),
-                    rhs_scale=g_scales[g][:],
+                    rhs=g_codes[g][:, first : first + N].bitcast(E5),
+                    rhs_scale=g_scales[g][:, first : first + N],
                     start=(g == 0),
                     stop=(g == PASSES - 1),
                 )
-            for n0, n1 in pieces(c):
-                scopy(res[c][:, n0:n1], acc[:, n0:n1])
+            return acc
 
-        def pieces(c):
-            return [(0, N // 2), (N // 2, N)] if c == 0 else [(0, N)]
+        def unload(c, acc, n0=0, n1=N, shift=0):
+            scopy(res[c][:, n0:n1], acc[:, shift + n0 : shift + n1])
 
-        def scatter(c):
+        def scatter(c, n0=0, n1=N):
+            vcopy(windows[c % 3][:].indirect(offsets[:, n0 // 16 : n1 // 16]), res[c][:, n0:n1])
+
+        def store(c):
             win = windows[c % 3]
-            for n0, n1 in pieces(c):
-                vcopy(win[:].indirect(offsets[:, n0 // 16 : n1 // 16]), res[c][:, n0:n1])
             if c + 1 < CHUNKS:
                 nc.sync.dma_start(out=out[P * c : P * (c + 1), :], in_=win[:])
             else:
                 nc.sync.dma_start(out=out[P * c : P * (c + 1), 0 : T // 2], in_=win[:, 0 : T // 2])
                 nc.scalar.dma_start(out=out[P * c : P * (c + 1), T // 2 : T], in_=win[:, T // 2 : T])
 
-        weigh_y(0)
-        weigh_y(1)
+        H = N // 2
+        Q = N // 4
+        for i in range(4):
+            weigh_y(i)
         scores(0)
         scores(1)
+        cast_x(scopy, 1, 2, 4)
         scores(2)
-        cast_x(vcopy, 1, x1_raw, 0, 128)
-        recip(0, 2)
         scores(3)
-        weigh_y(2)
-        weigh_y(3)
+        cast_x(vcopy, 1, 0, 2)
+        recip(0, 2)
+        quant_x(1, 0, 2)
         coefs(0, 2)
-        quant_x(1, 0, 4)
-        grad(0)
+        quant_x(1, 2, 4)
         recip(2, 2)
-        grad(1)
         scores(4)
-        scores(5)
-        scores(6)
         coefs(2, 2)
-        scores(7)
-        weigh_y(4)
-        weigh_y(5)
-        weigh_y(6)
-        weigh_y(7)
-        grad(2)
+        for i in range(5, 8):
+            scores(i)
+        for i in range(4):
+            grad(i)
+        for i in range(4, 8):
+            weigh_y(i)
         recip(4, 2)
-        grad(3)
+        cast_m(vcopy, 0, [0])
         coefs(4, 2)
-        weave_g(vcopy, 0, 0, 128)
         recip(6, 2)
-        weave_g(scopy, 0, 128, 512)
-        stage_m(0, 1, "early")
-        cast_m(scopy, 0)
-        grad(4)
+        cast_m(vcopy, 0, [1])
         coefs(6, 2)
-        grad(5)
-        grad(6)
-        grad(7)
-        quant_g(0)
-        weave_g(vcopy, 1, 0, 320)
-        weave_g(scopy, 1, 320, 512)
-        quant_m(0, 1)
-        quant_g(1)
-        product(0)
-        stage_m(1, 3, "late")
+        weave_g(scopy, 0, 0, Q)
+        weave_g(scopy, 0, Q, H)
+        for i in range(4, 8):
+            grad(i, 0, H)
+        quant_m(0)
+        weave_g(vcopy, 1, 0, H)
+        quant_g(0, 0, H)
+        quant_g(1, 0, H)
         cast_m(scopy, 1)
-        cast_m(vcopy, 2)
-        quant_m(1, 3)
-        product(1)
-        scatter(0)
-        stage_m(3, 4, "late")
+        unload(0, product(0, 0), 0, H, PAD)
+        for i in range(4, 8):
+            grad(i, H, N)
+        quant_m(1)
+        early = product(1, 0)
+        for g in range(PASSES):
+            weave_g(scopy, g, H, H + Q)
+            weave_g(scopy, g, H + Q, N)
+        unload(1, early, 0, H, PAD)
+        quant_g(0, H, N)
+        scatter(0, 0, H)
+        quant_g(1, H, N)
+        cast_m(scopy, 2)
+        scatter(1, 0, H)
+        quant_m(2)
+        for c in range(2):
+            unload(c, product(c), H, N)
+            scatter(c, H, N)
+            store(c)
         cast_m(scopy, 3)
-        quant_m(3, 4)
-        product(2)
-        scatter(1)
-        product(3)
-        scatter(2)
-        scatter(3)
+        quant_m(3)
+        for c in range(2, CHUNKS):
+            unload(c, product(c))
+            scatter(c)
+            store(c)

@@ -33,8 +33,7 @@ def tile_attend_gkl_w_kernel(tc, xT, wT, y, wt, xm, offs, out):
     with ExitStack() as ctx:
         held = ctx.enter_context(tc.tile_pool(name="held", bufs=1))
         sb = ctx.enter_context(tc.tile_pool(name="sb", bufs=1))
-        ps_s = ctx.enter_context(tc.psum_pool(name="ps_s", bufs=4))
-        ps_o = ctx.enter_context(tc.psum_pool(name="ps_o", bufs=4))
+        psum = ctx.enter_context(tc.psum_pool(name="psum", bufs=8))
 
         offsets = held.tile([P, N // 16], U16, name="offsets")
         x_raw = [sb.tile([P, PACK, 512], F32, name=f"x_raw{g}") for g in range(PASSES)]
@@ -59,9 +58,9 @@ def tile_attend_gkl_w_kernel(tc, xT, wT, y, wt, xm, offs, out):
         nc.sync.dma_start(out=y_raw[0][:, 0:2, :], in_=rows(y, 0)[:, 0:2, :])
         nc.sync.dma_start(out=y_raw[0][:, 2:4, :], in_=rows(y, 0)[:, 2:4, :])
         nc.sync.dma_start(out=x_raw[1][:], in_=x_planes[:, :, 512:1024])
+        nc.sync.dma_start(out=m_raw[0][:], in_=rows(xm, 0))
         nc.sync.dma_start(out=y_raw[1][:], in_=rows(y, 1))
-        for g in range(PASSES):
-            nc.sync.dma_start(out=m_raw[g][:], in_=rows(xm, g))
+        nc.sync.dma_start(out=m_raw[1][:], in_=rows(xm, 1))
 
         nc.vector.memset(windows[0][:], 0.0)
         nc.vector.memset(windows[1][:], 0.0)
@@ -122,7 +121,7 @@ def tile_attend_gkl_w_kernel(tc, xT, wT, y, wt, xm, offs, out):
         def scores(i):
             g, t = divmod(i, PACK)
             cols = slice(P * t, P * (t + 1))
-            acc = ps_s.tile([P, N], F32, name="acc")
+            acc = psum.tile([P, N], F32, name="acc", tag="bank")
             nc.tensor.matmul_mx(
                 out=acc[:],
                 lhsT=x_codes[g][:, cols].bitcast(E4),
@@ -153,6 +152,43 @@ def tile_attend_gkl_w_kernel(tc, xT, wT, y, wt, xm, offs, out):
                 out=yw[g][:, t, :], in0=y_raw[g][:, t, :], scalar1=wt_sb[:, g, t : t + 1], scalar2=0.0,
                 op0=ALU.mult, op1=ALU.add,
             )
+
+        gap = sb.tile([P, PACK, PAD], F32, name="gap")
+        neg_coef = sb.tile([P, PACK], F32, name="neg_coef")
+
+        def weigh_y_late(i):
+            g, t = divmod(i, PACK)
+            nc.scalar.activation(
+                out=yw[g][:, t, PAD:N], in_=y_raw[g][:, t, PAD:N], func=ACT.Copy, scale=wt_sb[:, g, t : t + 1]
+            )
+
+        def gap_first(t):
+            nc.vector.scalar_tensor_tensor(
+                out=gap[:, t, :], in0=y_raw[1][:, t, 0:PAD], scalar=sums[:, PACK + t : PACK + t + 1], in1=e_sb[1][:, t, 0:PAD],
+                op0=ALU.mult, op1=ALU.subtract,
+            )
+
+        def neg_coefs():
+            nc.vector.scalar_tensor_tensor(
+                out=neg_coef[:], in0=inv[:, PACK : 2 * PACK], scalar=-1.0, in1=wt_sb[:, 1, 0:PACK], op0=ALU.mult, op1=ALU.mult
+            )
+
+        def grad_first():
+            nc.vector.tensor_tensor(
+                out=g_bf[1][:, 0:PAD, :].rearrange("p (c i) t -> p c t i", i=2),
+                in0=gap[:].rearrange("p t (c i) -> p c t i", i=2),
+                in1=neg_coef[:].unsqueeze(1).unsqueeze(3).to_broadcast([P, PAD // 2, PACK, 2]),
+                op=ALU.mult,
+            )
+
+        def neg_grad_late(t):
+            nc.vector.scalar_tensor_tensor(
+                out=planes(1, PAD, N)[:, t, :], in0=e_sb[1][:, t, PAD:N], scalar=neg_coef[:, t : t + 1], in1=yw[1][:, t, PAD:N],
+                op0=ALU.mult, op1=ALU.add,
+            )
+
+        def negate(o, i):
+            nc.scalar.activation(out=o, in_=i, func=ACT.Copy, scale=-1.0)
 
         def recip(i, n):
             nc.vector.reciprocal(out=inv[:, i : i + n], in_=sums[:, i : i + n])
@@ -199,7 +235,7 @@ def tile_attend_gkl_w_kernel(tc, xT, wT, y, wt, xm, offs, out):
             )
 
         def product(c, first=PAD):
-            acc = ps_o.tile([P, N], F32, name="acc_o")
+            acc = psum.tile([P, N], F32, name="acc_o", tag="bank")
             for g in range(PASSES):
                 cols = slice(P * (PASSES * c + g), P * (PASSES * c + g + 1))
                 nc.tensor.matmul_mx(
@@ -248,31 +284,29 @@ def tile_attend_gkl_w_kernel(tc, xT, wT, y, wt, xm, offs, out):
             scores(i)
         for i in range(4):
             grad(i)
-        for i in range(4, 8):
-            weigh_y(i)
-        recip(4, 2)
-        cast_m(vcopy, 0, [0])
-        coefs(4, 2)
-        recip(6, 2)
-        cast_m(vcopy, 0, [1])
-        coefs(6, 2)
         weave_g(scopy, 0, 0, Q)
         weave_g(scopy, 0, Q, H)
-        for i in range(4, 8):
-            grad(i, 0, H)
-        quant_m(0)
-        weave_g(vcopy, 1, 0, H)
+        cast_m(scopy, 0)
+        recip(4, 4)
+        gap_first(0)
+        neg_coefs()
+        for t in range(1, PACK):
+            gap_first(t)
         quant_g(0, 0, H)
+        grad_first()
+        quant_m(0)
         quant_g(1, 0, H)
-        cast_m(scopy, 1)
         unload(0, product(0, 0), 0, H, PAD)
         for i in range(4, 8):
-            grad(i, H, N)
+            weigh_y_late(i)
+        cast_m(scopy, 1)
+        for t in range(PACK):
+            neg_grad_late(t)
         quant_m(1)
         early = product(1, 0)
-        for g in range(PASSES):
-            weave_g(scopy, g, H, H + Q)
-            weave_g(scopy, g, H + Q, N)
+        for g, copy in enumerate([scopy, negate]):
+            weave_g(copy, g, H, H + Q)
+            weave_g(copy, g, H + Q, N)
         unload(1, early, 0, H, PAD)
         quant_g(0, H, N)
         scatter(0, 0, H)

@@ -4,9 +4,12 @@ import concourse.mybir as mybir
 
 D, T, R, N = 512, 2048, 1024, 512
 P, PACK = 128, 4
-PASSES = R // (P * PACK)
+K_PASS = P * PACK
+PASSES = R // K_PASS
 CHUNKS = D // P
-PAD = N // 2
+HALF = N // 2
+EARLY_CHUNKS = 2
+WINDOWS = 3
 FLOPS = 2 * 2 * D * R * N
 
 F32 = mybir.dt.float32
@@ -23,12 +26,25 @@ AX = mybir.AxisListType
 
 def tile_attend_gkl_w_kernel(tc, xT, wT, y, wt, xm, offs, out):
     nc = tc.nc
+    early, late = slice(0, HALF), slice(HALF, N)
 
-    def vcopy(o, i):
-        nc.vector.tensor_copy(out=o, in_=i)
+    def vcopy(dst, src):
+        nc.vector.tensor_copy(out=dst, in_=src)
 
-    def scopy(o, i):
-        nc.scalar.copy(out=o, in_=i)
+    def scopy(dst, src):
+        nc.scalar.copy(out=dst, in_=src)
+
+    def scale_rows(dst, src, factor):
+        nc.scalar.activation(out=dst, in_=src, func=ACT.Copy, scale=factor)
+
+    def woven_view(ap, run):
+        return ap.rearrange("p (c i) t -> p c t i", i=run)
+
+    def planes_view(ap, run):
+        return ap.rearrange("p t (c i) -> p c t i", i=run)
+
+    def weave(dst, src):
+        scopy(woven_view(dst, 4), planes_view(src, 4))
 
     with ExitStack() as ctx:
         held = ctx.enter_context(tc.tile_pool(name="held", bufs=1))
@@ -36,39 +52,47 @@ def tile_attend_gkl_w_kernel(tc, xT, wT, y, wt, xm, offs, out):
         psum = ctx.enter_context(tc.psum_pool(name="psum", bufs=8))
 
         offsets = held.tile([P, N // 16], U16, name="offsets")
-        x_raw = [sb.tile([P, PACK, 512], F32, name=f"x_raw{g}") for g in range(PASSES)]
+        x_raw = [sb.tile([P, PACK, K_PASS], F32, name=f"x_raw{g}") for g in range(PASSES)]
         w_raw = [sb.tile([P, T], F32, name=f"w_raw{j}") for j in range(PACK)]
         y_raw = [sb.tile([P, PACK, N], F32, name=f"y_raw{g}") for g in range(PASSES)]
-        m_raw = [sb.tile([P, PACK, D], F32, name=f"m_raw{g}") for g in range(PASSES)]
+        m_raw = [[sb.tile([P, PACK, D // 2], F32, name=f"m_raw{g}_{h}") for h in range(2)] for g in range(PASSES)]
         wt_sb = sb.tile([P, PASSES, 8], F32, name="wt_sb")
-        windows = [sb.tile([P, T], F32, name=f"window{c}") for c in range(3)]
+        windows = [sb.tile([P, T], F32, name=f"window{c}") for c in range(WINDOWS)]
 
         x_planes = xT[0].rearrange("(p j) r -> p j r", j=PACK)
         w_planes = wT.rearrange("(p j) c -> p j c", j=PACK)
 
         def rows(ap, g):
-            return ap[0, 512 * g : 512 * (g + 1), :].rearrange("(p t) n -> p t n", t=PACK)
+            return ap[0, K_PASS * g : K_PASS * (g + 1), :].rearrange("(p t) n -> p t n", t=PACK)
+
+        def load_x(g):
+            nc.sync.dma_start(out=x_raw[g][:], in_=x_planes[:, :, K_PASS * g : K_PASS * (g + 1)])
+
+        def load_m(g, h):
+            nc.sync.dma_start(out=m_raw[g][h][:], in_=rows(xm, g)[:, :, D // 2 * h : D // 2 * (h + 1)])
 
         nc.sync.dma_start(out=w_raw[0][:], in_=w_planes[:, 0, :])
         nc.sync.dma_start(offsets[:], offs)
         for j in range(1, PACK):
             nc.sync.dma_start(out=w_raw[j][:], in_=w_planes[:, j, :])
-        nc.sync.dma_start(out=x_raw[0][:], in_=x_planes[:, :, 0:512])
+        load_x(0)
         nc.sync.dma_start(out=wt_sb[:, :, 0:PACK], in_=wt[0].rearrange("(g p t) o -> p g (t o)", g=PASSES, t=PACK))
-        nc.sync.dma_start(out=y_raw[0][:, 0:2, :], in_=rows(y, 0)[:, 0:2, :])
-        nc.sync.dma_start(out=y_raw[0][:, 2:4, :], in_=rows(y, 0)[:, 2:4, :])
-        nc.sync.dma_start(out=x_raw[1][:], in_=x_planes[:, :, 512:1024])
-        nc.sync.dma_start(out=m_raw[0][:], in_=rows(xm, 0))
+        for t in range(0, PACK, 2):
+            nc.sync.dma_start(out=y_raw[0][:, t : t + 2, :], in_=rows(y, 0)[:, t : t + 2, :])
+        load_x(1)
+        load_m(0, 0)
         nc.sync.dma_start(out=y_raw[1][:], in_=rows(y, 1))
-        nc.sync.dma_start(out=m_raw[1][:], in_=rows(xm, 1))
+        load_m(1, 0)
+        for g in range(PASSES):
+            load_m(g, 1)
 
         nc.vector.memset(windows[0][:], 0.0)
         nc.vector.memset(windows[1][:], 0.0)
         nc.gpsimd.memset(windows[2][:], 0.0)
 
-        x_bf = [sb.tile([P, 2048], BF16, name=f"x_bf{g}", align_bytes=64) for g in range(PASSES)]
-        x_codes = [sb.tile([P, 512], U32, name=f"x_codes{g}", align_bytes=64) for g in range(PASSES)]
-        x_scales = [sb.tile([P, 512], U8, name=f"x_scales{g}", align_bytes=64) for g in range(PASSES)]
+        x_bf = [sb.tile([P, K_PASS * PACK], BF16, name=f"x_bf{g}", align_bytes=64) for g in range(PASSES)]
+        x_codes = [sb.tile([P, K_PASS], U32, name=f"x_codes{g}", align_bytes=64) for g in range(PASSES)]
+        x_scales = [sb.tile([P, K_PASS], U8, name=f"x_scales{g}", align_bytes=64) for g in range(PASSES)]
 
         def cast_x(copy, g, t0, t1):
             copy(
@@ -80,7 +104,7 @@ def tile_attend_gkl_w_kernel(tc, xT, wT, y, wt, xm, offs, out):
             nc.vector.quantize_mx(
                 out=x_codes[g][:, P * t0 : P * t1].bitcast(E4),
                 scales=x_scales[g][:, P * t0 : P * t1],
-                in_=x_bf[g][:, 512 * t0 : 512 * t1],
+                in_=x_bf[g][:, P * PACK * t0 : P * PACK * t1],
             )
 
         w_bf = sb.tile([P, N, PACK], BF16, name="w_bf", align_bytes=64)
@@ -98,28 +122,10 @@ def tile_attend_gkl_w_kernel(tc, xT, wT, y, wt, xm, offs, out):
         neg_max = sb.tile([P, PASSES * PACK], F32, name="neg_max")
         sums = sb.tile([P, PASSES * PACK], F32, name="sums")
         inv = sb.tile([P, PASSES * PACK], F32, name="inv")
-        coef = sb.tile([P, PASSES * PACK], F32, name="coef")
         e_sb = [sb.tile([P, PACK, N], F32, name=f"e_sb{g}") for g in range(PASSES)]
-        yw = [sb.tile([P, PACK, N], F32, name=f"yw{g}") for g in range(PASSES)]
-        g_pl0 = sb.tile([P, PACK, N], BF16, name="g_pl0")
-        g_pl1 = [sb.tile([P, PACK, N // 2], BF16, name=f"g_pl1_{h}") for h in range(2)]
 
-        def planes(g, n0, n1):
-            if g == 0:
-                return g_pl0[:, :, n0:n1]
-            h = n0 // (N // 2)
-            return g_pl1[h][:, :, n0 - h * (N // 2) : n1 - h * (N // 2)]
-
-        g_bf = [sb.tile([P, N, PACK], BF16, name=f"g_bf{g}", align_bytes=64) for g in range(PASSES)]
-        g_codes = [sb.tile([P, PAD + N], U32, name=f"g_codes{g}", align_bytes=64) for g in range(PASSES)]
-        g_scales = [sb.tile([P, PAD + N], U8, name=f"g_scales{g}", align_bytes=64) for g in range(PASSES)]
-
-        for g in range(PASSES):
-            nc.vector.memset(g_codes[g][:, 0:PAD], 0)
-            nc.vector.memset(g_scales[g][:, 0:PAD], 0)
-
-        def scores(i):
-            g, t = divmod(i, PACK)
+        def scores(g, t):
+            i = PACK * g + t
             cols = slice(P * t, P * (t + 1))
             acc = psum.tile([P, N], F32, name="acc", tag="bank")
             nc.tensor.matmul_mx(
@@ -136,85 +142,70 @@ def tile_attend_gkl_w_kernel(tc, xT, wT, y, wt, xm, offs, out):
                 out=e_sb[g][:, t, :], in_=acc[:], func=ACT.Exp, bias=neg_max[:, i : i + 1], accum_out=sums[:, i : i + 1]
             )
 
-        def weigh_y(i):
-            g, t = divmod(i, PACK)
-            nc.scalar.activation(out=yw[g][:, t, :], in_=y_raw[g][:, t, :], func=ACT.Copy, scale=wt_sb[:, g, t : t + 1])
+        def recip(g, t0, t1):
+            cols = slice(PACK * g + t0, PACK * g + t1)
+            nc.vector.reciprocal(out=inv[:, cols], in_=sums[:, cols])
 
-        def weigh_y_vec(i):
-            g, t = divmod(i, PACK)
-            nc.vector.tensor_scalar(
-                out=yw[g][:, t, :], in0=y_raw[g][:, t, :], scalar1=wt_sb[:, g, t : t + 1], scalar2=None, op0=ALU.mult
+        g_bf = [sb.tile([P, N, PACK], BF16, name=f"g_bf{g}", align_bytes=64) for g in range(PASSES)]
+        g_codes = [sb.tile([P, HALF + N], U32, name=f"g_codes{g}", align_bytes=64) for g in range(PASSES)]
+        g_scales = [sb.tile([P, HALF + N], U8, name=f"g_scales{g}", align_bytes=64) for g in range(PASSES)]
+        for g in range(PASSES):
+            nc.vector.memset(g_codes[g][:, 0:HALF], 0)
+            nc.vector.memset(g_scales[g][:, 0:HALF], 0)
+
+        def quant_g(g, half):
+            cols = slice(HALF + half.start, HALF + half.stop)
+            nc.vector.quantize_mx(
+                out=g_codes[g][:, cols].bitcast(E5),
+                scales=g_scales[g][:, cols],
+                in_=g_bf[g][:, half, :].rearrange("p n t -> p (n t)"),
             )
 
-        def weigh_y_pool(i):
-            g, t = divmod(i, PACK)
-            nc.gpsimd.tensor_scalar(
-                out=yw[g][:, t, :], in0=y_raw[g][:, t, :], scalar1=wt_sb[:, g, t : t + 1], scalar2=0.0,
-                op0=ALU.mult, op1=ALU.add,
-            )
+        coef = sb.tile([P, PACK], F32, name="coef")
+        yw = sb.tile([P, PACK, N], F32, name="yw")
+        g_planes = sb.tile([P, PACK, N], BF16, name="g_planes")
 
-        gap = sb.tile([P, PACK, PAD], F32, name="gap")
-        neg_coef = sb.tile([P, PACK], F32, name="neg_coef")
+        def coefs(t0, t1):
+            nc.vector.tensor_tensor(out=coef[:, t0:t1], in0=inv[:, t0:t1], in1=wt_sb[:, 0, t0:t1], op=ALU.mult)
 
-        def weigh_y_late(i):
-            g, t = divmod(i, PACK)
-            nc.scalar.activation(
-                out=yw[g][:, t, PAD:N], in_=y_raw[g][:, t, PAD:N], func=ACT.Copy, scale=wt_sb[:, g, t : t + 1]
-            )
-
-        def gap_first(t):
+        def grad_plane(t):
             nc.vector.scalar_tensor_tensor(
-                out=gap[:, t, :], in0=y_raw[1][:, t, 0:PAD], scalar=sums[:, PACK + t : PACK + t + 1], in1=e_sb[1][:, t, 0:PAD],
+                out=g_planes[:, t, :], in0=e_sb[0][:, t, :], scalar=coef[:, t : t + 1], in1=yw[:, t, :],
                 op0=ALU.mult, op1=ALU.subtract,
             )
 
-        def neg_coefs():
+        def weave_planes(half):
+            for n0 in range(half.start, half.stop, HALF // 2):
+                cols = slice(n0, n0 + HALF // 2)
+                weave(g_bf[0][:, cols, :], g_planes[:, :, cols])
+
+        neg_wt = sb.tile([P, PACK], F32, name="neg_wt")
+        neg_coef = sb.tile([P, PACK], F32, name="neg_coef")
+        excess = sb.tile([P, PACK, HALF], F32, name="excess")
+        neg_yw = sb.tile([P, PACK, HALF], F32, name="neg_yw")
+        neg_pw = sb.tile([P, PACK, HALF], F32, name="neg_pw")
+        scale_rows(neg_wt[:], wt_sb[:, 1, 0:PACK], -1.0)
+
+        def excess_plane(t):
             nc.vector.scalar_tensor_tensor(
-                out=neg_coef[:], in0=inv[:, PACK : 2 * PACK], scalar=-1.0, in1=wt_sb[:, 1, 0:PACK], op0=ALU.mult, op1=ALU.mult
+                out=excess[:, t, :], in0=y_raw[1][:, t, early], scalar=sums[:, PACK + t : PACK + t + 1],
+                in1=e_sb[1][:, t, early], op0=ALU.mult, op1=ALU.subtract,
             )
 
-        def grad_first():
+        def grad_early():
             nc.vector.tensor_tensor(
-                out=g_bf[1][:, 0:PAD, :].rearrange("p (c i) t -> p c t i", i=2),
-                in0=gap[:].rearrange("p t (c i) -> p c t i", i=2),
-                in1=neg_coef[:].unsqueeze(1).unsqueeze(3).to_broadcast([P, PAD // 2, PACK, 2]),
+                out=woven_view(g_bf[1][:, early, :], 2),
+                in0=planes_view(excess[:], 2),
+                in1=neg_coef[:].unsqueeze(1).unsqueeze(3).to_broadcast([P, HALF // 2, PACK, 2]),
                 op=ALU.mult,
             )
 
-        def neg_grad_late(t):
-            nc.vector.scalar_tensor_tensor(
-                out=planes(1, PAD, N)[:, t, :], in0=e_sb[1][:, t, PAD:N], scalar=neg_coef[:, t : t + 1], in1=yw[1][:, t, PAD:N],
-                op0=ALU.mult, op1=ALU.add,
-            )
-
-        def negate(o, i):
-            nc.scalar.activation(out=o, in_=i, func=ACT.Copy, scale=-1.0)
-
-        def recip(i, n):
-            nc.vector.reciprocal(out=inv[:, i : i + n], in_=sums[:, i : i + n])
-
-        def coefs(i, n):
-            g, t = divmod(i, PACK)
-            nc.vector.tensor_tensor(out=coef[:, i : i + n], in0=inv[:, i : i + n], in1=wt_sb[:, g, t : t + n], op=ALU.mult)
-
-        def grad(i, n0=0, n1=N):
-            g, t = divmod(i, PACK)
-            nc.vector.scalar_tensor_tensor(
-                out=planes(g, n0, n1)[:, t, :], in0=e_sb[g][:, t, n0:n1], scalar=coef[:, i : i + 1], in1=yw[g][:, t, n0:n1],
-                op0=ALU.mult, op1=ALU.subtract,
-            )
-
-        def interleave(copy, dst, src):
-            copy(dst.rearrange("p (c i) t -> p c t i", i=4), src.rearrange("p t (c i) -> p c t i", i=4))
-
-        def weave_g(copy, g, n0, n1):
-            interleave(copy, g_bf[g][:, n0:n1, :], planes(g, n0, n1))
-
-        def quant_g(g, n0, n1):
-            nc.vector.quantize_mx(
-                out=g_codes[g][:, PAD + n0 : PAD + n1].bitcast(E5),
-                scales=g_scales[g][:, PAD + n0 : PAD + n1],
-                in_=g_bf[g][:, n0:n1, :].rearrange("p n t -> p (n t)"),
+        def grad_late():
+            nc.vector.tensor_tensor(
+                out=woven_view(g_bf[1][:, late, :], 2),
+                in0=planes_view(neg_yw[:], 2),
+                in1=planes_view(neg_pw[:], 2),
+                op=ALU.subtract,
             )
 
         m_bf = [sb.tile([P, PASSES, P, PACK], BF16, name=f"m_bf{c}", tag="m_bf", bufs=2, align_bytes=64) for c in range(CHUNKS)]
@@ -222,9 +213,10 @@ def tile_attend_gkl_w_kernel(tc, xT, wT, y, wt, xm, offs, out):
         m_scales = sb.tile([P, CHUNKS * PASSES * P], U8, name="m_scales", align_bytes=64)
         res = [sb.tile([P, N], F32, name=f"res{c}") for c in range(CHUNKS)]
 
-        def cast_m(copy, c, passes=range(PASSES)):
-            for g in passes:
-                interleave(copy, m_bf[c][:, g, :, :], m_raw[g][:, :, P * c : P * (c + 1)])
+        def cast_m(c):
+            h, k = divmod(c, CHUNKS // 2)
+            for g in range(PASSES):
+                weave(m_bf[c][:, g, :, :], m_raw[g][h][:, :, P * k : P * (k + 1)])
 
         def quant_m(c):
             cols = slice(PASSES * P * c, PASSES * P * (c + 1))
@@ -234,8 +226,8 @@ def tile_attend_gkl_w_kernel(tc, xT, wT, y, wt, xm, offs, out):
                 in_=m_bf[c][:].rearrange("p g d t -> p (g d t)"),
             )
 
-        def product(c, first=PAD):
-            acc = psum.tile([P, N], F32, name="acc_o", tag="bank")
+        def product(c, first):
+            acc = psum.tile([P, N], F32, name="acc_out", tag="bank")
             for g in range(PASSES):
                 cols = slice(P * (PASSES * c + g), P * (PASSES * c + g + 1))
                 nc.tensor.matmul_mx(
@@ -249,78 +241,76 @@ def tile_attend_gkl_w_kernel(tc, xT, wT, y, wt, xm, offs, out):
                 )
             return acc
 
-        def unload(c, acc, n0=0, n1=N, shift=0):
-            scopy(res[c][:, n0:n1], acc[:, shift + n0 : shift + n1])
+        def early_product(c):
+            return product(c, 0)[:, HALF:N]
 
-        def scatter(c, n0=0, n1=N):
-            vcopy(windows[c % 3][:].indirect(offsets[:, n0 // 16 : n1 // 16]), res[c][:, n0:n1])
+        def scatter(c, slots):
+            entries = offsets[:, slots.start // 16 : slots.stop // 16]
+            vcopy(windows[c % WINDOWS][:].indirect(entries), res[c][:, slots])
 
         def store(c):
-            win = windows[c % 3]
+            win = windows[c % WINDOWS]
             if c + 1 < CHUNKS:
                 nc.sync.dma_start(out=out[P * c : P * (c + 1), :], in_=win[:])
             else:
                 nc.sync.dma_start(out=out[P * c : P * (c + 1), 0 : T // 2], in_=win[:, 0 : T // 2])
                 nc.scalar.dma_start(out=out[P * c : P * (c + 1), T // 2 : T], in_=win[:, T // 2 : T])
 
-        H = N // 2
-        Q = N // 4
-        for i in range(4):
-            weigh_y(i)
-        scores(0)
-        scores(1)
-        cast_x(scopy, 1, 2, 4)
-        scores(2)
-        scores(3)
+        def finish(c, slots):
+            scopy(res[c][:, slots], product(c, HALF)[:, slots])
+            scatter(c, slots)
+            store(c)
+
+        for t in range(PACK):
+            scale_rows(yw[:, t, :], y_raw[0][:, t, :], wt_sb[:, 0, t : t + 1])
+        for t in range(PACK):
+            scores(0, t)
         cast_x(vcopy, 1, 0, 2)
-        recip(0, 2)
+        recip(0, 0, 2)
+        cast_x(vcopy, 1, 2, 4)
         quant_x(1, 0, 2)
         coefs(0, 2)
         quant_x(1, 2, 4)
-        recip(2, 2)
-        scores(4)
-        coefs(2, 2)
-        for i in range(5, 8):
-            scores(i)
-        for i in range(4):
-            grad(i)
-        weave_g(scopy, 0, 0, Q)
-        weave_g(scopy, 0, Q, H)
-        cast_m(scopy, 0)
-        recip(4, 4)
-        gap_first(0)
-        neg_coefs()
+        recip(0, 2, 4)
+        scores(1, 0)
+        coefs(2, 4)
         for t in range(1, PACK):
-            gap_first(t)
-        quant_g(0, 0, H)
-        grad_first()
-        quant_m(0)
-        quant_g(1, 0, H)
-        unload(0, product(0, 0), 0, H, PAD)
-        for i in range(4, 8):
-            weigh_y_late(i)
-        cast_m(scopy, 1)
+            scores(1, t)
         for t in range(PACK):
-            neg_grad_late(t)
+            grad_plane(t)
+
+        cast_m(0)
+        weave_planes(early)
+        recip(1, 0, PACK)
+        excess_plane(0)
+        nc.vector.tensor_tensor(out=neg_coef[:], in0=inv[:, PACK : 2 * PACK], in1=neg_wt[:], op=ALU.mult)
+        for t in range(1, PACK):
+            excess_plane(t)
+        quant_m(0)
+        quant_g(0, early)
+        grad_early()
+        quant_g(1, early)
+        scopy(res[0][:, early], early_product(0))
+
+        for t in range(PACK):
+            scale_rows(neg_yw[:, t, :], y_raw[1][:, t, late], neg_wt[:, t : t + 1])
+        for t in range(PACK):
+            scale_rows(neg_pw[:, t, :], e_sb[1][:, t, late], neg_coef[:, t : t + 1])
+        cast_m(1)
+        grad_late()
         quant_m(1)
-        early = product(1, 0)
-        for g, copy in enumerate([scopy, negate]):
-            weave_g(copy, g, H, H + Q)
-            weave_g(copy, g, H + Q, N)
-        unload(1, early, 0, H, PAD)
-        quant_g(0, H, N)
-        scatter(0, 0, H)
-        quant_g(1, H, N)
-        cast_m(scopy, 2)
-        scatter(1, 0, H)
+        quant_g(1, late)
+        sums_1 = early_product(1)
+        weave_planes(late)
+        scopy(res[1][:, early], sums_1)
+        scatter(0, early)
+        quant_g(0, late)
+        cast_m(2)
+        scatter(1, early)
         quant_m(2)
-        for c in range(2):
-            unload(c, product(c), H, N)
-            scatter(c, H, N)
-            store(c)
-        cast_m(scopy, 3)
+        for c in range(EARLY_CHUNKS):
+            finish(c, late)
+        cast_m(3)
         quant_m(3)
-        for c in range(2, CHUNKS):
-            unload(c, product(c))
-            scatter(c)
-            store(c)
+        for c in range(EARLY_CHUNKS, CHUNKS):
+            finish(c, slice(0, N))

@@ -52,9 +52,12 @@ def tile_attend_gkl_w_kernel(tc, xT, wT, y, wt, xm, offs, out):
         psum = ctx.enter_context(tc.psum_pool(name="psum", bufs=8))
 
         offsets = held.tile([P, N // 16], U16, name="offsets")
-        x_raw = [sb.tile([P, PACK, K_PASS], F32, name=f"x_raw{g}") for g in range(PASSES)]
+        x_head = [sb.tile([P, PACK, K_PASS // 2], F32, name=f"x_head{h}") for h in range(2)]
+        x_tail = sb.tile([P, PACK, K_PASS], F32, name="x_tail")
         w_raw = [sb.tile([P, T], F32, name=f"w_raw{j}") for j in range(PACK)]
-        y_raw = [sb.tile([P, PACK, N], F32, name=f"y_raw{g}") for g in range(PASSES)]
+        y_raw = sb.tile([P, PACK, N], F32, name="y_raw")
+        y_early = sb.tile([P, PACK, HALF], F32, name="y_early")
+        y_late = sb.tile([P, PACK, HALF], F32, name="y_late")
         m_raw = [[sb.tile([P, PACK, D // 2], F32, name=f"m_raw{g}_{h}") for h in range(2)] for g in range(PASSES)]
         wt_sb = sb.tile([P, PASSES, 8], F32, name="wt_sb")
         windows = [sb.tile([P, T], F32, name=f"window{c}") for c in range(WINDOWS)]
@@ -65,8 +68,8 @@ def tile_attend_gkl_w_kernel(tc, xT, wT, y, wt, xm, offs, out):
         def rows(ap, g):
             return ap[0, K_PASS * g : K_PASS * (g + 1), :].rearrange("(p t) n -> p t n", t=PACK)
 
-        def load_x(g):
-            nc.sync.dma_start(out=x_raw[g][:], in_=x_planes[:, :, K_PASS * g : K_PASS * (g + 1)])
+        def load_y(t0, t1):
+            nc.sync.dma_start(out=y_raw[:, t0:t1, :], in_=rows(y, 0)[:, t0:t1, :])
 
         def load_m(g, h):
             nc.sync.dma_start(out=m_raw[g][h][:], in_=rows(xm, g)[:, :, D // 2 * h : D // 2 * (h + 1)])
@@ -75,13 +78,16 @@ def tile_attend_gkl_w_kernel(tc, xT, wT, y, wt, xm, offs, out):
         nc.sync.dma_start(offsets[:], offs)
         for j in range(1, PACK):
             nc.sync.dma_start(out=w_raw[j][:], in_=w_planes[:, j, :])
-        load_x(0)
+        for h in range(2):
+            nc.sync.dma_start(out=x_head[h][:], in_=x_planes[:, :, K_PASS // 2 * h : K_PASS // 2 * (h + 1)])
         nc.sync.dma_start(out=wt_sb[:, :, 0:PACK], in_=wt[0].rearrange("(g p t) o -> p g (t o)", g=PASSES, t=PACK))
-        for t in range(0, PACK, 2):
-            nc.sync.dma_start(out=y_raw[0][:, t : t + 2, :], in_=rows(y, 0)[:, t : t + 2, :])
-        load_x(1)
+        load_y(0, 2)
+        load_y(2, 3)
+        nc.sync.dma_start(out=x_tail[:], in_=x_planes[:, :, K_PASS:R])
+        load_y(3, 4)
         load_m(0, 0)
-        nc.sync.dma_start(out=y_raw[1][:], in_=rows(y, 1))
+        nc.sync.dma_start(out=y_late[:], in_=rows(y, 1)[:, :, late])
+        nc.sync.dma_start(out=y_early[:], in_=rows(y, 1)[:, :, early])
         load_m(1, 0)
         for g in range(PASSES):
             load_m(g, 1)
@@ -94,10 +100,10 @@ def tile_attend_gkl_w_kernel(tc, xT, wT, y, wt, xm, offs, out):
         x_codes = [sb.tile([P, K_PASS], U32, name=f"x_codes{g}", align_bytes=64) for g in range(PASSES)]
         x_scales = [sb.tile([P, K_PASS], U8, name=f"x_scales{g}", align_bytes=64) for g in range(PASSES)]
 
-        def cast_x(copy, g, t0, t1):
+        def cast_x(copy, g, t0, t1, raw=x_tail, m0=0, m1=P):
             copy(
-                x_bf[g][:].rearrange("p (t m j) -> p m j t", t=PACK, j=PACK)[:, :, :, t0:t1],
-                x_raw[g][:].rearrange("p j (m t) -> p m j t", t=PACK)[:, :, :, t0:t1],
+                x_bf[g][:].rearrange("p (t m j) -> p m j t", t=PACK, j=PACK)[:, m0:m1, :, t0:t1],
+                raw[:].rearrange("p j (m t) -> p m j t", t=PACK)[:, :, :, t0:t1],
             )
 
         def quant_x(g, t0, t1):
@@ -110,11 +116,18 @@ def tile_attend_gkl_w_kernel(tc, xT, wT, y, wt, xm, offs, out):
         w_bf = sb.tile([P, N, PACK], BF16, name="w_bf", align_bytes=64)
         w_codes = sb.tile([P, N], U32, name="w_codes", align_bytes=64)
         w_scales = sb.tile([P, N], U8, name="w_scales", align_bytes=64)
-        for j in range(PACK):
+        for j in range(PACK - 1):
             vcopy(w_bf[:, :, j], w_raw[j][:].indirect(offsets[:]))
-        nc.vector.quantize_mx(out=w_codes[:].bitcast(E4), scales=w_scales[:], in_=w_bf[:].rearrange("p n j -> p (n j)"))
-        cast_x(vcopy, 0, 0, 2)
-        cast_x(scopy, 0, 2, 4)
+        for half in (early, late):
+            vcopy(w_bf[:, half, PACK - 1], w_raw[PACK - 1][:].indirect(offsets[:, half.start // 16 : half.stop // 16]))
+        for half in (early, late):
+            nc.vector.quantize_mx(
+                out=w_codes[:, half].bitcast(E4), scales=w_scales[:, half], in_=w_bf[:, half, :].rearrange("p n j -> p (n j)")
+            )
+        cast_x(scopy, 0, 0, 2, x_head[0], 0, P // 2)
+        cast_x(scopy, 0, 2, 4, x_head[0], 0, P // 2)
+        cast_x(vcopy, 0, 0, 2, x_head[1], P // 2, P)
+        cast_x(scopy, 0, 2, 4, x_head[1], P // 2, P)
         quant_x(0, 0, 1)
         quant_x(0, 1, 2)
         quant_x(0, 2, 4)
@@ -165,6 +178,9 @@ def tile_attend_gkl_w_kernel(tc, xT, wT, y, wt, xm, offs, out):
         yw = sb.tile([P, PACK, N], F32, name="yw")
         g_planes = sb.tile([P, PACK, N], BF16, name="g_planes")
 
+        def weigh_y(t):
+            scale_rows(yw[:, t, :], y_raw[:, t, :], wt_sb[:, 0, t : t + 1])
+
         def coefs(t0, t1):
             nc.vector.tensor_tensor(out=coef[:, t0:t1], in0=inv[:, t0:t1], in1=wt_sb[:, 0, t0:t1], op=ALU.mult)
 
@@ -188,7 +204,7 @@ def tile_attend_gkl_w_kernel(tc, xT, wT, y, wt, xm, offs, out):
 
         def excess_plane(t):
             nc.vector.scalar_tensor_tensor(
-                out=excess[:, t, :], in0=y_raw[1][:, t, early], scalar=sums[:, PACK + t : PACK + t + 1],
+                out=excess[:, t, :], in0=y_early[:, t, :], scalar=sums[:, PACK + t : PACK + t + 1],
                 in1=e_sb[1][:, t, early], op0=ALU.mult, op1=ALU.subtract,
             )
 
@@ -261,10 +277,11 @@ def tile_attend_gkl_w_kernel(tc, xT, wT, y, wt, xm, offs, out):
             scatter(c, slots)
             store(c)
 
-        for t in range(PACK):
-            scale_rows(yw[:, t, :], y_raw[0][:, t, :], wt_sb[:, 0, t : t + 1])
+        for t in range(PACK - 1):
+            weigh_y(t)
         for t in range(PACK):
             scores(0, t)
+        weigh_y(PACK - 1)
         cast_x(vcopy, 1, 0, 2)
         recip(0, 0, 2)
         cast_x(vcopy, 1, 2, 4)
@@ -293,7 +310,7 @@ def tile_attend_gkl_w_kernel(tc, xT, wT, y, wt, xm, offs, out):
         scopy(res[0][:, early], early_product(0))
 
         for t in range(PACK):
-            scale_rows(neg_yw[:, t, :], y_raw[1][:, t, late], neg_wt[:, t : t + 1])
+            scale_rows(neg_yw[:, t, :], y_late[:, t, :], neg_wt[:, t : t + 1])
         for t in range(PACK):
             scale_rows(neg_pw[:, t, :], e_sb[1][:, t, late], neg_coef[:, t : t + 1])
         cast_m(1)

@@ -8,8 +8,6 @@ K_PASS = P * PACK
 PASSES = R // K_PASS
 CHUNKS = D // P
 HALF = N // 2
-EARLY_CHUNKS = 2
-WINDOWS = 3
 FLOPS = 2 * 2 * D * R * N
 
 F32 = mybir.dt.float32
@@ -43,9 +41,6 @@ def tile_attend_gkl_w_kernel(tc, xT, wT, y, wt, xm, offs, out):
     def planes_view(ap, run):
         return ap.rearrange("p t (c i) -> p c t i", i=run)
 
-    def weave(dst, src):
-        scopy(woven_view(dst, 4), planes_view(src, 4))
-
     with ExitStack() as ctx:
         held = ctx.enter_context(tc.tile_pool(name="held", bufs=1))
         sb = ctx.enter_context(tc.tile_pool(name="sb", bufs=1))
@@ -56,11 +51,10 @@ def tile_attend_gkl_w_kernel(tc, xT, wT, y, wt, xm, offs, out):
         x_tail = sb.tile([P, PACK, K_PASS], F32, name="x_tail")
         w_raw = [sb.tile([P, T], F32, name=f"w_raw{j}") for j in range(PACK)]
         y_raw = sb.tile([P, PACK, N], F32, name="y_raw")
-        y_early = sb.tile([P, PACK, HALF], F32, name="y_early")
-        y_late = sb.tile([P, PACK, HALF], F32, name="y_late")
-        m_raw = [[sb.tile([P, PACK, D // 2], F32, name=f"m_raw{g}_{h}") for h in range(2)] for g in range(PASSES)]
+        y_tail = sb.tile([P, PACK, N], F32, name="y_tail")
+        m_raw = [sb.tile([P, PACK, D], F32, name=f"m_raw{g}") for g in range(PASSES)]
         wt_sb = sb.tile([P, PASSES, 8], F32, name="wt_sb")
-        windows = [sb.tile([P, T], F32, name=f"window{c}") for c in range(WINDOWS)]
+        windows = [sb.tile([P, T], F32, name=f"window{c}") for c in range(CHUNKS)]
 
         x_planes = xT[0].rearrange("(p j) r -> p j r", j=PACK)
         w_planes = wT.rearrange("(p j) c -> p j c", j=PACK)
@@ -71,9 +65,6 @@ def tile_attend_gkl_w_kernel(tc, xT, wT, y, wt, xm, offs, out):
         def load_y(t0, t1):
             nc.sync.dma_start(out=y_raw[:, t0:t1, :], in_=rows(y, 0)[:, t0:t1, :])
 
-        def load_m(g, h):
-            nc.sync.dma_start(out=m_raw[g][h][:], in_=rows(xm, g)[:, :, D // 2 * h : D // 2 * (h + 1)])
-
         nc.sync.dma_start(out=w_raw[0][:], in_=w_planes[:, 0, :])
         nc.sync.dma_start(offsets[:], offs)
         for j in range(1, PACK):
@@ -82,19 +73,16 @@ def tile_attend_gkl_w_kernel(tc, xT, wT, y, wt, xm, offs, out):
             nc.sync.dma_start(out=x_head[h][:], in_=x_planes[:, :, K_PASS // 2 * h : K_PASS // 2 * (h + 1)])
         nc.sync.dma_start(out=wt_sb[:, :, 0:PACK], in_=wt[0].rearrange("(g p t) o -> p g (t o)", g=PASSES, t=PACK))
         load_y(0, 2)
-        load_y(2, 3)
         nc.sync.dma_start(out=x_tail[:], in_=x_planes[:, :, K_PASS:R])
-        load_y(3, 4)
-        load_m(0, 0)
-        nc.sync.dma_start(out=y_late[:], in_=rows(y, 1)[:, :, late])
-        nc.sync.dma_start(out=y_early[:], in_=rows(y, 1)[:, :, early])
-        load_m(1, 0)
+        load_y(2, 4)
+        nc.sync.dma_start(out=y_tail[:], in_=rows(y, 1))
         for g in range(PASSES):
-            load_m(g, 1)
+            nc.sync.dma_start(out=m_raw[g][:], in_=rows(xm, g))
 
         nc.vector.memset(windows[0][:], 0.0)
         nc.vector.memset(windows[1][:], 0.0)
-        nc.gpsimd.memset(windows[2][:], 0.0)
+        nc.vector.memset(windows[2][:], 0.0)
+        nc.gpsimd.memset(windows[3][:], 0.0)
 
         x_bf = [sb.tile([P, K_PASS * PACK], BF16, name=f"x_bf{g}", align_bytes=64) for g in range(PASSES)]
         x_codes = [sb.tile([P, K_PASS], U32, name=f"x_codes{g}", align_bytes=64) for g in range(PASSES)]
@@ -160,17 +148,13 @@ def tile_attend_gkl_w_kernel(tc, xT, wT, y, wt, xm, offs, out):
             nc.vector.reciprocal(out=inv[:, cols], in_=sums[:, cols])
 
         g_bf = [sb.tile([P, N, PACK], BF16, name=f"g_bf{g}", align_bytes=64) for g in range(PASSES)]
-        g_codes = [sb.tile([P, HALF + N], U32, name=f"g_codes{g}", align_bytes=64) for g in range(PASSES)]
-        g_scales = [sb.tile([P, HALF + N], U8, name=f"g_scales{g}", align_bytes=64) for g in range(PASSES)]
-        for g in range(PASSES):
-            nc.vector.memset(g_codes[g][:, 0:HALF], 0)
-            nc.vector.memset(g_scales[g][:, 0:HALF], 0)
+        g_codes = [sb.tile([P, N], U32, name=f"g_codes{g}", align_bytes=64) for g in range(PASSES)]
+        g_scales = [sb.tile([P, N], U8, name=f"g_scales{g}", align_bytes=64) for g in range(PASSES)]
 
         def quant_g(g, half):
-            cols = slice(HALF + half.start, HALF + half.stop)
             nc.vector.quantize_mx(
-                out=g_codes[g][:, cols].bitcast(E5),
-                scales=g_scales[g][:, cols],
+                out=g_codes[g][:, half].bitcast(E5),
+                scales=g_scales[g][:, half],
                 in_=g_bf[g][:, half, :].rearrange("p n t -> p (n t)"),
             )
 
@@ -190,10 +174,8 @@ def tile_attend_gkl_w_kernel(tc, xT, wT, y, wt, xm, offs, out):
                 op0=ALU.mult, op1=ALU.subtract,
             )
 
-        def weave_planes(half):
-            for n0 in range(half.start, half.stop, HALF // 2):
-                cols = slice(n0, n0 + HALF // 2)
-                weave(g_bf[0][:, cols, :], g_planes[:, :, cols])
+        def weave_planes(copy, cols):
+            copy(woven_view(g_bf[0][:, cols, :], 4), planes_view(g_planes[:, :, cols], 4))
 
         neg_wt = sb.tile([P, PACK], F32, name="neg_wt")
         neg_coef = sb.tile([P, PACK], F32, name="neg_coef")
@@ -204,7 +186,7 @@ def tile_attend_gkl_w_kernel(tc, xT, wT, y, wt, xm, offs, out):
 
         def excess_plane(t):
             nc.vector.scalar_tensor_tensor(
-                out=excess[:, t, :], in0=y_early[:, t, :], scalar=sums[:, PACK + t : PACK + t + 1],
+                out=excess[:, t, :], in0=y_tail[:, t, early], scalar=sums[:, PACK + t : PACK + t + 1],
                 in1=e_sb[1][:, t, early], op0=ALU.mult, op1=ALU.subtract,
             )
 
@@ -224,15 +206,14 @@ def tile_attend_gkl_w_kernel(tc, xT, wT, y, wt, xm, offs, out):
                 op=ALU.subtract,
             )
 
-        m_bf = [sb.tile([P, PASSES, P, PACK], BF16, name=f"m_bf{c}", tag="m_bf", bufs=2, align_bytes=64) for c in range(CHUNKS)]
+        m_bf = [sb.tile([P, PASSES, P, PACK], BF16, name=f"m_bf{c}", align_bytes=64) for c in range(CHUNKS)]
         m_codes = sb.tile([P, CHUNKS * PASSES * P], U32, name="m_codes", align_bytes=64)
         m_scales = sb.tile([P, CHUNKS * PASSES * P], U8, name="m_scales", align_bytes=64)
         res = [sb.tile([P, N], F32, name=f"res{c}") for c in range(CHUNKS)]
 
-        def cast_m(c):
-            h, k = divmod(c, CHUNKS // 2)
-            for g in range(PASSES):
-                weave(m_bf[c][:, g, :, :], m_raw[g][h][:, :, P * k : P * (k + 1)])
+        def cast_m(copy, c, passes=range(PASSES)):
+            for g in passes:
+                copy(woven_view(m_bf[c][:, g, :, :], 4), planes_view(m_raw[g][:, :, P * c : P * (c + 1)], 4))
 
         def quant_m(c):
             cols = slice(PASSES * P * c, PASSES * P * (c + 1))
@@ -242,92 +223,96 @@ def tile_attend_gkl_w_kernel(tc, xT, wT, y, wt, xm, offs, out):
                 in_=m_bf[c][:].rearrange("p g d t -> p (g d t)"),
             )
 
-        def product(c, first):
+        def product(c, slots):
             acc = psum.tile([P, N], F32, name="acc_out", tag="bank")
             for g in range(PASSES):
                 cols = slice(P * (PASSES * c + g), P * (PASSES * c + g + 1))
                 nc.tensor.matmul_mx(
-                    out=acc[:],
+                    out=acc[:, slots],
                     lhsT=m_codes[:, cols].bitcast(E4),
                     lhsT_scale=m_scales[:, cols],
-                    rhs=g_codes[g][:, first : first + N].bitcast(E5),
-                    rhs_scale=g_scales[g][:, first : first + N],
+                    rhs=g_codes[g][:, slots].bitcast(E5),
+                    rhs_scale=g_scales[g][:, slots],
                     start=(g == 0),
                     stop=(g == PASSES - 1),
                 )
-            return acc
+            return acc[:, slots]
 
-        def early_product(c):
-            return product(c, 0)[:, HALF:N]
+        def entries(slots):
+            return offsets[:, slots.start // 16 : slots.stop // 16]
 
-        def scatter(c, slots):
-            entries = offsets[:, slots.start // 16 : slots.stop // 16]
-            vcopy(windows[c % WINDOWS][:].indirect(entries), res[c][:, slots])
+        def vscatter(c, slots):
+            vcopy(windows[c][:].indirect(entries(slots)), res[c][:, slots])
 
-        def store(c):
-            win = windows[c % WINDOWS]
-            if c + 1 < CHUNKS:
-                nc.sync.dma_start(out=out[P * c : P * (c + 1), :], in_=win[:])
-            else:
-                nc.sync.dma_start(out=out[P * c : P * (c + 1), 0 : T // 2], in_=win[:, 0 : T // 2])
-                nc.scalar.dma_start(out=out[P * c : P * (c + 1), T // 2 : T], in_=win[:, T // 2 : T])
+        def sscatter(c, slots):
+            nc.scalar.activation(out=windows[c][:].indirect(entries(slots)), in_=res[c][:, slots], func=ACT.Copy)
 
-        def finish(c, slots):
-            scopy(res[c][:, slots], product(c, HALF)[:, slots])
-            scatter(c, slots)
-            store(c)
+        def store(c, queue=nc.sync):
+            queue.dma_start(out=out[P * c : P * (c + 1), :], in_=windows[c][:])
 
-        for t in range(PACK - 1):
-            weigh_y(t)
-        for t in range(PACK):
-            scores(0, t)
-        weigh_y(PACK - 1)
+        weigh_y(0)
+        weigh_y(1)
+        scores(0, 0)
+        scores(0, 1)
+        cast_x(scopy, 1, 2, 4)
+        scores(0, 2)
+        scores(0, 3)
+        weigh_y(2)
+        weigh_y(3)
         cast_x(vcopy, 1, 0, 2)
         recip(0, 0, 2)
-        cast_x(vcopy, 1, 2, 4)
         quant_x(1, 0, 2)
         coefs(0, 2)
         quant_x(1, 2, 4)
+        for t in range(PACK):
+            scores(1, t)
         recip(0, 2, 4)
-        scores(1, 0)
+        grad_plane(0)
         coefs(2, 4)
         for t in range(1, PACK):
-            scores(1, t)
-        for t in range(PACK):
             grad_plane(t)
 
-        cast_m(0)
-        weave_planes(early)
         recip(1, 0, PACK)
         excess_plane(0)
         nc.vector.tensor_tensor(out=neg_coef[:], in0=inv[:, PACK : 2 * PACK], in1=neg_wt[:], op=ALU.mult)
         for t in range(1, PACK):
             excess_plane(t)
-        quant_m(0)
-        quant_g(0, early)
-        grad_early()
-        quant_g(1, early)
-        scopy(res[0][:, early], early_product(0))
-
+        cast_m(scopy, 0, [0])
+        weave_planes(scopy, slice(0, HALF // 2))
         for t in range(PACK):
-            scale_rows(neg_yw[:, t, :], y_late[:, t, :], neg_wt[:, t : t + 1])
+            scale_rows(neg_yw[:, t, :], y_tail[:, t, late], neg_wt[:, t : t + 1])
+        cast_m(scopy, 0, [1])
         for t in range(PACK):
             scale_rows(neg_pw[:, t, :], e_sb[1][:, t, late], neg_coef[:, t : t + 1])
-        cast_m(1)
+        weave_planes(vcopy, slice(HALF // 2, HALF))
+        grad_early()
+        quant_g(0, early)
+        quant_g(1, early)
+        quant_m(0)
+
+        scopy(res[0][:, early], product(0, early))
+        sscatter(0, early)
+        weave_planes(vcopy, late)
         grad_late()
-        quant_m(1)
-        quant_g(1, late)
-        sums_1 = early_product(1)
-        weave_planes(late)
-        scopy(res[1][:, early], sums_1)
-        scatter(0, early)
         quant_g(0, late)
-        cast_m(2)
-        scatter(1, early)
+        quant_g(1, late)
+        scopy(res[0][:, late], product(0, late))
+        sscatter(0, late)
+        store(0)
+        every = slice(0, N)
+        cast_m(scopy, 1)
+        quant_m(1)
+        cast_m(vcopy, 2)
+        cast_m(vcopy, 3)
         quant_m(2)
-        for c in range(EARLY_CHUNKS):
-            finish(c, late)
-        cast_m(3)
         quant_m(3)
-        for c in range(EARLY_CHUNKS, CHUNKS):
-            finish(c, slice(0, N))
+        vcopy(res[1][:], product(1, every))
+        vscatter(1, every)
+        store(1)
+        scopy(res[2][:], product(2, every))
+        scopy(res[3][:], product(3, every))
+        sscatter(2, early)
+        sscatter(2, late)
+        store(2, nc.scalar)
+        vscatter(3, every)
+        store(3)

@@ -52,7 +52,7 @@ def tile_attend_gkl_w_kernel(tc, xT, wT, y, wt, xm, offs, out):
         w_raw = [sb.tile([P, T], F32, name=f"w_raw{j}") for j in range(PACK)]
         y_raw = sb.tile([P, PACK, N], F32, name="y_raw")
         y_tail = sb.tile([P, PACK, N], F32, name="y_tail")
-        m_raw = [sb.tile([P, PACK, D], F32, name=f"m_raw{g}") for g in range(PASSES)]
+        m_raw = [sb.tile([P, PASSES, PACK, D // 2], F32, name=f"m_raw{h}") for h in range(2)]
         wt_sb = sb.tile([P, PASSES, 8], F32, name="wt_sb")
         windows = [sb.tile([P, T], F32, name=f"window{c}") for c in range(CHUNKS)]
 
@@ -76,8 +76,9 @@ def tile_attend_gkl_w_kernel(tc, xT, wT, y, wt, xm, offs, out):
         nc.sync.dma_start(out=x_tail[:], in_=x_planes[:, :, K_PASS:R])
         load_y(2, 4)
         nc.sync.dma_start(out=y_tail[:], in_=rows(y, 1))
-        for g in range(PASSES):
-            nc.sync.dma_start(out=m_raw[g][:], in_=rows(xm, g))
+        for h in range(2):
+            for g in range(PASSES):
+                nc.sync.dma_start(out=m_raw[h][:, g, :, :], in_=rows(xm, g)[:, :, D // 2 * h : D // 2 * (h + 1)])
 
         nc.vector.memset(windows[0][:], 0.0)
         nc.vector.memset(windows[1][:], 0.0)
@@ -179,48 +180,46 @@ def tile_attend_gkl_w_kernel(tc, xT, wT, y, wt, xm, offs, out):
 
         neg_wt = sb.tile([P, PACK], F32, name="neg_wt")
         neg_coef = sb.tile([P, PACK], F32, name="neg_coef")
-        excess = sb.tile([P, PACK, HALF], F32, name="excess")
-        neg_yw = sb.tile([P, PACK, HALF], F32, name="neg_yw")
-        neg_pw = sb.tile([P, PACK, HALF], F32, name="neg_pw")
+        excess = sb.tile([P, PACK, N], F32, name="excess", tag="excess", align_bytes=64)
         scale_rows(neg_wt[:], wt_sb[:, 1, 0:PACK], -1.0)
 
-        def excess_plane(t):
+        def excess_plane(t, half):
             nc.vector.scalar_tensor_tensor(
-                out=excess[:, t, :], in0=y_tail[:, t, early], scalar=sums[:, PACK + t : PACK + t + 1],
-                in1=e_sb[1][:, t, early], op0=ALU.mult, op1=ALU.subtract,
+                out=excess[:, t, half], in0=y_tail[:, t, half], scalar=sums[:, PACK + t : PACK + t + 1],
+                in1=e_sb[1][:, t, half], op0=ALU.mult, op1=ALU.subtract,
             )
 
-        def grad_early():
+        def grad_woven(half):
             nc.vector.tensor_tensor(
-                out=woven_view(g_bf[1][:, early, :], 2),
-                in0=planes_view(excess[:], 2),
+                out=woven_view(g_bf[1][:, half, :], 2),
+                in0=planes_view(excess[:, :, half], 2),
                 in1=neg_coef[:].unsqueeze(1).unsqueeze(3).to_broadcast([P, HALF // 2, PACK, 2]),
                 op=ALU.mult,
             )
 
-        def grad_late():
-            nc.vector.tensor_tensor(
-                out=woven_view(g_bf[1][:, late, :], 2),
-                in0=planes_view(neg_yw[:], 2),
-                in1=planes_view(neg_pw[:], 2),
-                op=ALU.subtract,
-            )
-
-        m_bf = [sb.tile([P, PASSES, P, PACK], BF16, name=f"m_bf{c}", align_bytes=64) for c in range(CHUNKS)]
+        m_head = [sb.tile([P, PASSES, P, PACK], BF16, name=f"m_bf{c}", align_bytes=64) for c in range(2)]
+        m_tail = sb.tile([P, 2, PASSES, P, PACK], BF16, name="m_tail", tag="excess", align_bytes=64)
+        m_bf = [m_head[0][:], m_head[1][:], m_tail[:, 0], m_tail[:, 1]]
         m_codes = sb.tile([P, CHUNKS * PASSES * P], U32, name="m_codes", align_bytes=64)
         m_scales = sb.tile([P, CHUNKS * PASSES * P], U8, name="m_scales", align_bytes=64)
-        res = [sb.tile([P, N], F32, name=f"res{c}") for c in range(CHUNKS)]
+        res_0 = sb.tile([P, N], F32, name="res_0", tag="res")
+        res_1 = sb.tile([P, N], F32, name="res_1")
+        res_tail = sb.tile([P, 2, N], F32, name="res_tail", tag="res")
+        res = [res_0[:], res_1[:], res_tail[:, 0], res_tail[:, 1]]
 
-        def cast_m(copy, c, passes=range(PASSES)):
-            for g in passes:
-                copy(woven_view(m_bf[c][:, g, :, :], 4), planes_view(m_raw[g][:, :, P * c : P * (c + 1)], 4))
+        def cast_m(copy, c):
+            h, k = divmod(c, CHUNKS // 2)
+            copy(
+                m_bf[c].rearrange("p g (c i) t -> p g c t i", i=4),
+                m_raw[h][:, :, :, P * k : P * (k + 1)].rearrange("p g t (c i) -> p g c t i", i=4),
+            )
 
         def quant_m(c):
             cols = slice(PASSES * P * c, PASSES * P * (c + 1))
             nc.vector.quantize_mx(
                 out=m_codes[:, cols].bitcast(E4),
                 scales=m_scales[:, cols],
-                in_=m_bf[c][:].rearrange("p g d t -> p (g d t)"),
+                in_=m_bf[c].rearrange("p g d t -> p (g d t)"),
             )
 
         def product(c, slots):
@@ -272,45 +271,41 @@ def tile_attend_gkl_w_kernel(tc, xT, wT, y, wt, xm, offs, out):
         for t in range(1, PACK):
             grad_plane(t)
 
+        cast_m(scopy, 0)
+        weave_planes(scopy, early)
+        weave_planes(scopy, late)
+        cast_m(scopy, 1)
         recip(1, 0, PACK)
-        excess_plane(0)
+        excess_plane(0, early)
         nc.vector.tensor_tensor(out=neg_coef[:], in0=inv[:, PACK : 2 * PACK], in1=neg_wt[:], op=ALU.mult)
         for t in range(1, PACK):
-            excess_plane(t)
-        cast_m(scopy, 0, [0])
-        weave_planes(scopy, slice(0, HALF // 2))
-        for t in range(PACK):
-            scale_rows(neg_yw[:, t, :], y_tail[:, t, late], neg_wt[:, t : t + 1])
-        cast_m(scopy, 0, [1])
-        for t in range(PACK):
-            scale_rows(neg_pw[:, t, :], e_sb[1][:, t, late], neg_coef[:, t : t + 1])
-        weave_planes(vcopy, slice(HALF // 2, HALF))
-        grad_early()
+            excess_plane(t, early)
+        quant_m(0)
+        grad_woven(early)
         quant_g(0, early)
         quant_g(1, early)
-        quant_m(0)
-
         scopy(res[0][:, early], product(0, early))
         sscatter(0, early)
-        weave_planes(vcopy, late)
-        grad_late()
+
+        for t in range(PACK):
+            excess_plane(t, late)
+        grad_woven(late)
         quant_g(0, late)
         quant_g(1, late)
         scopy(res[0][:, late], product(0, late))
         sscatter(0, late)
-        store(0)
+        store(0, nc.scalar)
         every = slice(0, N)
-        cast_m(scopy, 1)
         quant_m(1)
         cast_m(vcopy, 2)
         cast_m(vcopy, 3)
         quant_m(2)
         quant_m(3)
-        vcopy(res[1][:], product(1, every))
+        vcopy(res[1], product(1, every))
         vscatter(1, every)
         store(1)
-        scopy(res[2][:], product(2, every))
-        scopy(res[3][:], product(3, every))
+        scopy(res[2], product(2, every))
+        scopy(res[3], product(3, every))
         sscatter(2, early)
         sscatter(2, late)
         store(2, nc.scalar)

@@ -197,21 +197,17 @@ def tile_attend_gkl_w_kernel(tc, xT, wT, y, wt, xm, offs, out):
                 op=ALU.mult,
             )
 
-        m_head = [sb.tile([P, PASSES, P, PACK], BF16, name=f"m_bf{c}", align_bytes=64) for c in range(2)]
-        m_tail = sb.tile([P, 2, PASSES, P, PACK], BF16, name="m_tail", tag="excess", align_bytes=64)
-        m_bf = [m_head[0][:], m_head[1][:], m_tail[:, 0], m_tail[:, 1]]
+        m_bf = [sb.tile([P, PASSES, P, PACK], BF16, name=f"m_bf{c}", align_bytes=64) for c in range(CHUNKS - 1)]
+        m_bf.append(sb.tile([P, PASSES, P, PACK], BF16, name="m_bf3", tag="excess", align_bytes=64))
         m_codes = sb.tile([P, CHUNKS * PASSES * P], U32, name="m_codes", align_bytes=64)
         m_scales = sb.tile([P, CHUNKS * PASSES * P], U8, name="m_scales", align_bytes=64)
-        res_0 = sb.tile([P, N], F32, name="res_0", tag="res")
-        res_1 = sb.tile([P, N], F32, name="res_1")
-        res_tail = sb.tile([P, 2, N], F32, name="res_tail", tag="res")
-        res = [res_0[:], res_1[:], res_tail[:, 0], res_tail[:, 1]]
+        res = [sb.tile([P, N], F32, name=f"res{c}") for c in range(CHUNKS)]
 
-        def cast_m(copy, c):
+        def cast_m(copy, c, passes=slice(0, PASSES)):
             h, k = divmod(c, CHUNKS // 2)
             copy(
-                m_bf[c].rearrange("p g (c i) t -> p g c t i", i=4),
-                m_raw[h][:, :, :, P * k : P * (k + 1)].rearrange("p g t (c i) -> p g c t i", i=4),
+                m_bf[c][:, passes].rearrange("p g (c i) t -> p g c t i", i=4),
+                m_raw[h][:, passes, :, P * k : P * (k + 1)].rearrange("p g t (c i) -> p g c t i", i=4),
             )
 
         def quant_m(c):
@@ -219,12 +215,15 @@ def tile_attend_gkl_w_kernel(tc, xT, wT, y, wt, xm, offs, out):
             nc.vector.quantize_mx(
                 out=m_codes[:, cols].bitcast(E4),
                 scales=m_scales[:, cols],
-                in_=m_bf[c].rearrange("p g d t -> p (g d t)"),
+                in_=m_bf[c][:].rearrange("p g d t -> p (g d t)"),
             )
 
-        def product(c, slots):
-            acc = psum.tile([P, N], F32, name="acc_out", tag="bank")
-            for g in range(PASSES):
+        def bank():
+            return psum.tile([P, N], F32, name="acc_out", tag="bank")
+
+        def product(c, slots, acc):
+            order = [0, 1] if c == 0 else [1, 0]
+            for g in order:
                 cols = slice(P * (PASSES * c + g), P * (PASSES * c + g + 1))
                 nc.tensor.matmul_mx(
                     out=acc[:, slots],
@@ -232,8 +231,8 @@ def tile_attend_gkl_w_kernel(tc, xT, wT, y, wt, xm, offs, out):
                     lhsT_scale=m_scales[:, cols],
                     rhs=g_codes[g][:, slots].bitcast(E5),
                     rhs_scale=g_scales[g][:, slots],
-                    start=(g == 0),
-                    stop=(g == PASSES - 1),
+                    start=(g == order[0]),
+                    stop=(g == order[-1]),
                 )
             return acc[:, slots]
 
@@ -271,43 +270,49 @@ def tile_attend_gkl_w_kernel(tc, xT, wT, y, wt, xm, offs, out):
         for t in range(1, PACK):
             grad_plane(t)
 
+        every = slice(0, N)
         cast_m(scopy, 0)
         weave_planes(scopy, early)
-        weave_planes(scopy, late)
         cast_m(scopy, 1)
+        weave_planes(scopy, late)
+        cast_m(scopy, 2, slice(0, 1))
         recip(1, 0, PACK)
-        excess_plane(0, early)
+        excess_plane(0, every)
         nc.vector.tensor_tensor(out=neg_coef[:], in0=inv[:, PACK : 2 * PACK], in1=neg_wt[:], op=ALU.mult)
-        for t in range(1, PACK):
-            excess_plane(t, early)
+        excess_plane(1, every)
+        excess_plane(2, early)
+        excess_plane(3, early)
         quant_m(0)
         grad_woven(early)
         quant_g(0, early)
         quant_g(1, early)
-        scopy(res[0][:, early], product(0, early))
+        scopy(res[0][:, early], product(0, early, bank()))
         sscatter(0, early)
-
-        for t in range(PACK):
-            excess_plane(t, late)
+        excess_plane(2, late)
+        excess_plane(3, late)
+        quant_m(1)
+        acc_1 = bank()
+        product(1, early, acc_1)
         grad_woven(late)
         quant_g(0, late)
         quant_g(1, late)
-        scopy(res[0][:, late], product(0, late))
+        scopy(res[0][:, late], product(0, late, bank()))
         sscatter(0, late)
-        store(0, nc.scalar)
-        every = slice(0, N)
-        quant_m(1)
-        cast_m(vcopy, 2)
+        store(0)
+        product(1, late, acc_1)
         cast_m(vcopy, 3)
+        cast_m(vcopy, 2, slice(1, 2))
         quant_m(2)
+        vcopy(res[1][:], acc_1[:])
         quant_m(3)
-        vcopy(res[1], product(1, every))
         vscatter(1, every)
         store(1)
-        scopy(res[2], product(2, every))
-        scopy(res[3], product(3, every))
+        acc_2 = product(2, every, bank())
+        for half in (early, late):
+            scopy(res[2][:, half], acc_2[:, half])
         sscatter(2, early)
         sscatter(2, late)
         store(2, nc.scalar)
+        vcopy(res[3][:], product(3, every, bank()))
         vscatter(3, every)
         store(3)

@@ -7,6 +7,8 @@ P, PACK = 128, 4
 K_PASS = P * PACK
 PASSES = R // K_PASS
 CHUNKS = D // P
+PIECES = CHUNKS * PASSES
+HEAD_PIECES = 5
 HALF = N // 2
 FLOPS = 2 * 2 * D * R * N
 
@@ -193,36 +195,43 @@ def tile_attend_gkl_w_kernel(tc, xT, wT, y, wt, xm, offs, out):
             nc.vector.tensor_tensor(
                 out=woven_view(g_bf[1][:, half, :], 2),
                 in0=planes_view(excess[:, :, half], 2),
-                in1=neg_coef[:].unsqueeze(1).unsqueeze(3).to_broadcast([P, HALF // 2, PACK, 2]),
+                in1=neg_coef[:].unsqueeze(1).unsqueeze(3).to_broadcast([P, (half.stop - half.start) // 2, PACK, 2]),
                 op=ALU.mult,
             )
 
-        m_bf = [sb.tile([P, PASSES, P, PACK], BF16, name=f"m_bf{c}", align_bytes=64) for c in range(CHUNKS - 1)]
-        m_bf.append(sb.tile([P, PASSES, P, PACK], BF16, name="m_bf3", tag="excess", align_bytes=64))
+        m_head = sb.tile([P, HEAD_PIECES, P, PACK], BF16, name="m_head", align_bytes=64)
+        m_tail = sb.tile([P, PIECES - HEAD_PIECES, P, PACK], BF16, name="m_tail", tag="excess", align_bytes=64)
         m_codes = sb.tile([P, CHUNKS * PASSES * P], U32, name="m_codes", align_bytes=64)
         m_scales = sb.tile([P, CHUNKS * PASSES * P], U8, name="m_scales", align_bytes=64)
-        res = [sb.tile([P, N], F32, name=f"res{c}") for c in range(CHUNKS)]
+        res_early = [sb.tile([P, HALF], F32, name=f"res_early{c}") for c in range(CHUNKS)]
+        res_late = [sb.tile([P, HALF], F32, name=f"res_late{c}", tag="res_late", bufs=2) for c in range(CHUNKS)]
 
-        def cast_m(copy, c, passes=slice(0, PASSES)):
+        def m_bf(c, g0, g1):
+            first = PASSES * c + g0
+            if first < HEAD_PIECES:
+                return m_head[:, first : first + g1 - g0]
+            return m_tail[:, first - HEAD_PIECES : first - HEAD_PIECES + g1 - g0]
+
+        def cast_m(copy, c, g0=0, g1=PASSES):
             h, k = divmod(c, CHUNKS // 2)
             copy(
-                m_bf[c][:, passes].rearrange("p g (c i) t -> p g c t i", i=4),
-                m_raw[h][:, passes, :, P * k : P * (k + 1)].rearrange("p g t (c i) -> p g c t i", i=4),
+                m_bf(c, g0, g1).rearrange("p g (c i) t -> p g c t i", i=4),
+                m_raw[h][:, g0:g1, :, P * k : P * (k + 1)].rearrange("p g t (c i) -> p g c t i", i=4),
             )
 
-        def quant_m(c):
-            cols = slice(PASSES * P * c, PASSES * P * (c + 1))
+        def quant_m(c, g0=0, g1=PASSES):
+            cols = slice(P * (PASSES * c + g0), P * (PASSES * c + g1))
             nc.vector.quantize_mx(
                 out=m_codes[:, cols].bitcast(E4),
                 scales=m_scales[:, cols],
-                in_=m_bf[c][:].rearrange("p g d t -> p (g d t)"),
+                in_=m_bf(c, g0, g1).rearrange("p g d t -> p (g d t)"),
             )
 
         def bank():
             return psum.tile([P, N], F32, name="acc_out", tag="bank")
 
         def product(c, slots, acc):
-            order = [0, 1] if c == 0 else [1, 0]
+            order = [1, 0] if c > 0 and slots == late else [0, 1]
             for g in order:
                 cols = slice(P * (PASSES * c + g), P * (PASSES * c + g + 1))
                 nc.tensor.matmul_mx(
@@ -239,14 +248,14 @@ def tile_attend_gkl_w_kernel(tc, xT, wT, y, wt, xm, offs, out):
         def entries(slots):
             return offsets[:, slots.start // 16 : slots.stop // 16]
 
-        def vscatter(c, slots):
-            vcopy(windows[c][:].indirect(entries(slots)), res[c][:, slots])
+        def scatter_early(c):
+            nc.scalar.activation(out=windows[c][:].indirect(entries(early)), in_=res_early[c][:], func=ACT.Copy)
 
-        def sscatter(c, slots):
-            nc.scalar.activation(out=windows[c][:].indirect(entries(slots)), in_=res[c][:, slots], func=ACT.Copy)
+        def scatter_late(c):
+            vcopy(windows[c][:].indirect(entries(late)), res_late[c][:])
 
-        def store(c, queue=nc.sync):
-            queue.dma_start(out=out[P * c : P * (c + 1), :], in_=windows[c][:])
+        def store(c):
+            nc.sync.dma_start(out=out[P * c : P * (c + 1), :], in_=windows[c][:])
 
         weigh_y(0)
         weigh_y(1)
@@ -275,7 +284,7 @@ def tile_attend_gkl_w_kernel(tc, xT, wT, y, wt, xm, offs, out):
         weave_planes(scopy, early)
         cast_m(scopy, 1)
         weave_planes(scopy, late)
-        cast_m(scopy, 2, slice(0, 1))
+        cast_m(scopy, 2, 0, 1)
         recip(1, 0, PACK)
         excess_plane(0, every)
         nc.vector.tensor_tensor(out=neg_coef[:], in0=inv[:, PACK : 2 * PACK], in1=neg_wt[:], op=ALU.mult)
@@ -286,33 +295,34 @@ def tile_attend_gkl_w_kernel(tc, xT, wT, y, wt, xm, offs, out):
         grad_woven(early)
         quant_g(0, early)
         quant_g(1, early)
-        scopy(res[0][:, early], product(0, early, bank()))
-        sscatter(0, early)
+        quant_m(1)
+        for c in (0, 1):
+            scopy(res_early[c][:], product(c, early, bank()))
+        for c in (0, 1):
+            scatter_early(c)
         excess_plane(2, late)
         excess_plane(3, late)
-        quant_m(1)
-        acc_1 = bank()
-        product(1, early, acc_1)
-        grad_woven(late)
         quant_g(0, late)
-        quant_g(1, late)
-        scopy(res[0][:, late], product(0, late, bank()))
-        sscatter(0, late)
-        store(0)
-        product(1, late, acc_1)
+        quarters = [slice(HALF, HALF + P), slice(HALF + P, N)]
+        for slots in quarters:
+            grad_woven(slots)
+        quant_g(1, quarters[0])
+        quant_m(2, 0, 1)
+        quant_g(1, quarters[1])
+        cast_m(vcopy, 2, 1, 2)
         cast_m(vcopy, 3)
-        cast_m(vcopy, 2, slice(1, 2))
-        quant_m(2)
-        vcopy(res[1][:], acc_1[:])
+        quant_m(2, 1, 2)
+        vcopy(res_late[0][:], product(0, late, bank()))
+        scatter_late(0)
+        store(0)
         quant_m(3)
-        vscatter(1, every)
+        vcopy(res_late[1][:], product(1, late, bank()))
+        scatter_late(1)
         store(1)
-        acc_2 = product(2, every, bank())
-        for half in (early, late):
-            scopy(res[2][:, half], acc_2[:, half])
-        sscatter(2, early)
-        sscatter(2, late)
-        store(2, nc.scalar)
-        vcopy(res[3][:], product(3, every, bank()))
-        vscatter(3, every)
-        store(3)
+        scopy(res_early[2][:], product(2, early, bank()))
+        vcopy(res_early[3][:], product(3, early, bank()))
+        for c in (2, 3):
+            scatter_early(c)
+            vcopy(res_late[c][:], product(c, late, bank()))
+            scatter_late(c)
+            store(c)

@@ -67,6 +67,10 @@ def tile_attend_gkl_w_kernel(tc, xT, wT, y, wt, xm, offs, out):
         def load_y(t0, t1):
             nc.sync.dma_start(out=y_raw[:, t0:t1, :], in_=rows(y, 0)[:, t0:t1, :])
 
+        def load_m(h):
+            for g in range(PASSES):
+                nc.sync.dma_start(out=m_raw[h][:, g, :, :], in_=rows(xm, g)[:, :, D // 2 * h : D // 2 * (h + 1)])
+
         nc.sync.dma_start(out=w_raw[0][:], in_=w_planes[:, 0, :])
         nc.sync.dma_start(offsets[:], offs)
         for j in range(1, PACK):
@@ -78,9 +82,8 @@ def tile_attend_gkl_w_kernel(tc, xT, wT, y, wt, xm, offs, out):
         nc.sync.dma_start(out=x_tail[:], in_=x_planes[:, :, K_PASS:R])
         load_y(2, 4)
         nc.sync.dma_start(out=y_tail[:], in_=rows(y, 1))
-        for h in range(2):
-            for g in range(PASSES):
-                nc.sync.dma_start(out=m_raw[h][:, g, :, :], in_=rows(xm, g)[:, :, D // 2 * h : D // 2 * (h + 1)])
+        load_m(0)
+        load_m(1)
 
         nc.vector.memset(windows[0][:], 0.0)
         nc.vector.memset(windows[1][:], 0.0)
@@ -303,24 +306,21 @@ def tile_attend_gkl_w_kernel(tc, xT, wT, y, wt, xm, offs, out):
         excess_plane(2, late)
         excess_plane(3, late)
         quant_g(0, late)
-        quarters = [slice(HALF, HALF + P), slice(HALF + P, N)]
-        for slots in quarters:
-            grad_woven(slots)
-        quant_g(1, quarters[0])
+        grad_woven(late)
         quant_m(2, 0, 1)
-        quant_g(1, quarters[1])
+        quant_g(1, late)
         cast_m(vcopy, 2, 1, 2)
         cast_m(vcopy, 3)
         quant_m(2, 1, 2)
         vcopy(res_late[0][:], product(0, late, bank()))
         scatter_late(0)
         store(0)
-        quant_m(3)
         vcopy(res_late[1][:], product(1, late, bank()))
+        quant_m(3)
         scatter_late(1)
         store(1)
         scopy(res_early[2][:], product(2, early, bank()))
-        vcopy(res_early[3][:], product(3, early, bank()))
+        scopy(res_early[3][:], product(3, early, bank()))
         for c in (2, 3):
             scatter_early(c)
             vcopy(res_late[c][:], product(c, late, bank()))

@@ -8,7 +8,7 @@ K_PASS = P * PACK
 PASSES = R // K_PASS
 CHUNKS = D // P
 PIECES = CHUNKS * PASSES
-HEAD_PIECES = 5
+HEAD_PIECES = 6
 HALF = N // 2
 FLOPS = 2 * 2 * D * R * N
 
@@ -67,9 +67,8 @@ def tile_attend_gkl_w_kernel(tc, xT, wT, y, wt, xm, offs, out):
         def load_y(t0, t1):
             nc.sync.dma_start(out=y_raw[:, t0:t1, :], in_=rows(y, 0)[:, t0:t1, :])
 
-        def load_m(h):
-            for g in range(PASSES):
-                nc.sync.dma_start(out=m_raw[h][:, g, :, :], in_=rows(xm, g)[:, :, D // 2 * h : D // 2 * (h + 1)])
+        def load_m(h, g):
+            nc.sync.dma_start(out=m_raw[h][:, g, :, :], in_=rows(xm, g)[:, :, D // 2 * h : D // 2 * (h + 1)])
 
         nc.sync.dma_start(out=w_raw[0][:], in_=w_planes[:, 0, :])
         nc.sync.dma_start(offsets[:], offs)
@@ -81,9 +80,11 @@ def tile_attend_gkl_w_kernel(tc, xT, wT, y, wt, xm, offs, out):
         load_y(0, 2)
         nc.sync.dma_start(out=x_tail[:], in_=x_planes[:, :, K_PASS:R])
         load_y(2, 4)
+        load_m(0, 0)
         nc.sync.dma_start(out=y_tail[:], in_=rows(y, 1))
-        load_m(0)
-        load_m(1)
+        load_m(0, 1)
+        for g in range(PASSES):
+            load_m(1, g)
 
         nc.vector.memset(windows[0][:], 0.0)
         nc.vector.memset(windows[1][:], 0.0)
@@ -207,7 +208,7 @@ def tile_attend_gkl_w_kernel(tc, xT, wT, y, wt, xm, offs, out):
         m_codes = sb.tile([P, CHUNKS * PASSES * P], U32, name="m_codes", align_bytes=64)
         m_scales = sb.tile([P, CHUNKS * PASSES * P], U8, name="m_scales", align_bytes=64)
         res_early = [sb.tile([P, HALF], F32, name=f"res_early{c}") for c in range(CHUNKS)]
-        res_late = [sb.tile([P, HALF], F32, name=f"res_late{c}", tag="res_late", bufs=2) for c in range(CHUNKS)]
+        res_late = [sb.tile([P, HALF], F32, name=f"res_late{c}") for c in range(CHUNKS)]
 
         def m_bf(c, g0, g1):
             first = PASSES * c + g0
@@ -222,6 +223,12 @@ def tile_attend_gkl_w_kernel(tc, xT, wT, y, wt, xm, offs, out):
                 m_raw[h][:, g0:g1, :, P * k : P * (k + 1)].rearrange("p g t (c i) -> p g c t i", i=4),
             )
 
+        def cast_m_pass(g):
+            scopy(
+                m_head[:, g : 2 * PASSES : PASSES].rearrange("p k (c i) t -> p k c t i", i=4),
+                m_raw[0][:, g].rearrange("p t (k c i) -> p k c t i", k=2, i=4),
+            )
+
         def quant_m(c, g0=0, g1=PASSES):
             cols = slice(P * (PASSES * c + g0), P * (PASSES * c + g1))
             nc.vector.quantize_mx(
@@ -234,7 +241,7 @@ def tile_attend_gkl_w_kernel(tc, xT, wT, y, wt, xm, offs, out):
             return psum.tile([P, N], F32, name="acc_out", tag="bank")
 
         def product(c, slots, acc):
-            order = [1, 0] if c > 0 and slots == late else [0, 1]
+            order = [1, 0] if c > 0 and slots != early else [0, 1]
             for g in order:
                 cols = slice(P * (PASSES * c + g), P * (PASSES * c + g + 1))
                 nc.tensor.matmul_mx(
@@ -264,13 +271,14 @@ def tile_attend_gkl_w_kernel(tc, xT, wT, y, wt, xm, offs, out):
         weigh_y(1)
         scores(0, 0)
         scores(0, 1)
-        cast_x(scopy, 1, 2, 4)
         scores(0, 2)
         scores(0, 3)
         weigh_y(2)
         weigh_y(3)
+        cast_m_pass(0)
         cast_x(vcopy, 1, 0, 2)
         recip(0, 0, 2)
+        cast_x(vcopy, 1, 2, 4)
         quant_x(1, 0, 2)
         coefs(0, 2)
         quant_x(1, 2, 4)
@@ -283,35 +291,31 @@ def tile_attend_gkl_w_kernel(tc, xT, wT, y, wt, xm, offs, out):
             grad_plane(t)
 
         every = slice(0, N)
-        cast_m(scopy, 0)
+        cast_m_pass(1)
         weave_planes(scopy, early)
-        cast_m(scopy, 1)
         weave_planes(scopy, late)
-        cast_m(scopy, 2, 0, 1)
+        cast_m(scopy, 2)
         recip(1, 0, PACK)
         excess_plane(0, every)
         nc.vector.tensor_tensor(out=neg_coef[:], in0=inv[:, PACK : 2 * PACK], in1=neg_wt[:], op=ALU.mult)
         excess_plane(1, every)
         excess_plane(2, early)
         excess_plane(3, early)
-        quant_m(0)
+        quant_m(0, 0, 2 * PASSES)
         grad_woven(early)
         quant_g(0, early)
         quant_g(1, early)
-        quant_m(1)
+        excess_plane(2, late)
+        excess_plane(3, late)
         for c in (0, 1):
             scopy(res_early[c][:], product(c, early, bank()))
         for c in (0, 1):
             scatter_early(c)
-        excess_plane(2, late)
-        excess_plane(3, late)
         quant_g(0, late)
         grad_woven(late)
-        quant_m(2, 0, 1)
+        quant_m(2)
         quant_g(1, late)
-        cast_m(vcopy, 2, 1, 2)
         cast_m(vcopy, 3)
-        quant_m(2, 1, 2)
         vcopy(res_late[0][:], product(0, late, bank()))
         scatter_late(0)
         store(0)
@@ -319,10 +323,10 @@ def tile_attend_gkl_w_kernel(tc, xT, wT, y, wt, xm, offs, out):
         quant_m(3)
         scatter_late(1)
         store(1)
-        scopy(res_early[2][:], product(2, early, bank()))
-        scopy(res_early[3][:], product(3, early, bank()))
         for c in (2, 3):
+            acc = product(c, every, bank())
+            scopy(res_early[c][:], acc[:, early])
+            scopy(res_late[c][:], acc[:, late])
             scatter_early(c)
-            vcopy(res_late[c][:], product(c, late, bank()))
             scatter_late(c)
             store(c)

@@ -34,6 +34,9 @@ def tile_attend_gkl_w_kernel(tc, xT, wT, y, wt, xm, offs, out):
     def scopy(dst, src):
         nc.scalar.copy(out=dst, in_=src)
 
+    def gcopy(dst, src):
+        nc.gpsimd.tensor_scalar(out=dst, in0=src, scalar1=1.0, scalar2=0.0, op0=ALU.mult, op1=ALU.add)
+
     def scale_rows(dst, src, factor):
         nc.scalar.activation(out=dst, in_=src, func=ACT.Copy, scale=factor)
 
@@ -50,11 +53,12 @@ def tile_attend_gkl_w_kernel(tc, xT, wT, y, wt, xm, offs, out):
 
         offsets = held.tile([P, N // 16], U16, name="offsets")
         x_head = [sb.tile([P, PACK, K_PASS // 2], F32, name=f"x_head{h}") for h in range(2)]
-        x_tail = sb.tile([P, PACK, K_PASS], F32, name="x_tail")
+        x_tail = [sb.tile([P, PACK, K_PASS // 2], F32, name=f"x_tail{h}") for h in range(2)]
         w_raw = [sb.tile([P, T], F32, name=f"w_raw{j}") for j in range(PACK)]
         y_raw = sb.tile([P, PACK, N], F32, name="y_raw")
         y_tail = sb.tile([P, PACK, N], F32, name="y_tail")
-        m_raw = [sb.tile([P, PASSES, PACK, D // 2], F32, name=f"m_raw{h}") for h in range(2)]
+        m_first = sb.tile([P, PASSES, PACK, D // 2], F32, name="m_first")
+        m_raw = {c: sb.tile([P, PASSES, PACK, P], F32, name=f"m_raw{c}", tag=f"m_raw{c}") for c in (2, 3)}
         wt_sb = sb.tile([P, PASSES, 8], F32, name="wt_sb")
         windows = [sb.tile([P, T], F32, name=f"window{c}") for c in range(CHUNKS)]
 
@@ -67,8 +71,8 @@ def tile_attend_gkl_w_kernel(tc, xT, wT, y, wt, xm, offs, out):
         def load_y(t0, t1):
             nc.sync.dma_start(out=y_raw[:, t0:t1, :], in_=rows(y, 0)[:, t0:t1, :])
 
-        def load_m(h, g):
-            nc.sync.dma_start(out=m_raw[h][:, g, :, :], in_=rows(xm, g)[:, :, D // 2 * h : D // 2 * (h + 1)])
+        def load_m(g):
+            nc.sync.dma_start(out=m_first[:, g, :, :], in_=rows(xm, g)[:, :, : D // 2])
 
         nc.sync.dma_start(out=w_raw[0][:], in_=w_planes[:, 0, :])
         nc.sync.dma_start(offsets[:], offs)
@@ -76,26 +80,29 @@ def tile_attend_gkl_w_kernel(tc, xT, wT, y, wt, xm, offs, out):
             nc.sync.dma_start(out=w_raw[j][:], in_=w_planes[:, j, :])
         for h in range(2):
             nc.sync.dma_start(out=x_head[h][:], in_=x_planes[:, :, K_PASS // 2 * h : K_PASS // 2 * (h + 1)])
+        for h in range(2):
+            first = K_PASS + K_PASS // 2 * h
+            nc.sync.dma_start(out=x_tail[h][:], in_=x_planes[:, :, first : first + K_PASS // 2])
         nc.sync.dma_start(out=wt_sb[:, :, 0:PACK], in_=wt[0].rearrange("(g p t) o -> p g (t o)", g=PASSES, t=PACK))
         load_y(0, 2)
-        nc.sync.dma_start(out=x_tail[:], in_=x_planes[:, :, K_PASS:R])
         load_y(2, 4)
-        load_m(0, 0)
         nc.sync.dma_start(out=y_tail[:], in_=rows(y, 1))
-        load_m(0, 1)
-        for g in range(PASSES):
-            load_m(1, g)
+        load_m(0)
+        load_m(1)
+        for c in (2, 3):
+            for g in range(PASSES):
+                nc.sync.dma_start(out=m_raw[c][:, g, :, :], in_=rows(xm, g)[:, :, P * c : P * (c + 1)])
 
         nc.vector.memset(windows[0][:], 0.0)
         nc.vector.memset(windows[1][:], 0.0)
         nc.vector.memset(windows[2][:], 0.0)
         nc.gpsimd.memset(windows[3][:], 0.0)
 
-        x_bf = [sb.tile([P, K_PASS * PACK], BF16, name=f"x_bf{g}", align_bytes=64) for g in range(PASSES)]
+        x_bf = [sb.tile([P, K_PASS * PACK], BF16, name=f"x_bf{g}", tag=f"cast{g}", align_bytes=64) for g in range(PASSES)]
         x_codes = [sb.tile([P, K_PASS], U32, name=f"x_codes{g}", align_bytes=64) for g in range(PASSES)]
-        x_scales = [sb.tile([P, K_PASS], U8, name=f"x_scales{g}", align_bytes=64) for g in range(PASSES)]
+        x_scales = [sb.tile([P, K_PASS], U8, name=f"x_scales{g}", tag=f"x_scales{g}", align_bytes=64) for g in range(PASSES)]
 
-        def cast_x(copy, g, t0, t1, raw=x_tail, m0=0, m1=P):
+        def cast_x(copy, g, t0, t1, raw, m0, m1):
             copy(
                 x_bf[g][:].rearrange("p (t m j) -> p m j t", t=PACK, j=PACK)[:, m0:m1, :, t0:t1],
                 raw[:].rearrange("p j (m t) -> p m j t", t=PACK)[:, :, :, t0:t1],
@@ -122,15 +129,20 @@ def tile_attend_gkl_w_kernel(tc, xT, wT, y, wt, xm, offs, out):
         cast_x(scopy, 0, 0, 2, x_head[0], 0, P // 2)
         cast_x(scopy, 0, 2, 4, x_head[0], 0, P // 2)
         cast_x(vcopy, 0, 0, 2, x_head[1], P // 2, P)
-        cast_x(scopy, 0, 2, 4, x_head[1], P // 2, P)
         quant_x(0, 0, 1)
+        cast_x(vcopy, 0, 2, 4, x_head[1], P // 2, P)
         quant_x(0, 1, 2)
         quant_x(0, 2, 4)
+        cast_x(scopy, 1, 0, 4, x_tail[0], 0, P // 2)
+        gcopy(
+            x_bf[1][:].rearrange("p (t m j) -> p m t j", t=PACK, j=PACK)[:, P // 2 :],
+            x_tail[1][:].rearrange("p j (m t) -> p m t j", t=PACK),
+        )
 
         neg_max = sb.tile([P, PASSES * PACK], F32, name="neg_max")
         sums = sb.tile([P, PASSES * PACK], F32, name="sums")
         inv = sb.tile([P, PASSES * PACK], F32, name="inv")
-        e_sb = [sb.tile([P, PACK, N], F32, name=f"e_sb{g}") for g in range(PASSES)]
+        e_sb = [sb.tile([P, PACK, N], F32, name=f"e_sb{g}", tag=f"e_sb{g}", align_bytes=64) for g in range(PASSES)]
 
         def scores(g, t):
             i = PACK * g + t
@@ -154,7 +166,7 @@ def tile_attend_gkl_w_kernel(tc, xT, wT, y, wt, xm, offs, out):
             cols = slice(PACK * g + t0, PACK * g + t1)
             nc.vector.reciprocal(out=inv[:, cols], in_=sums[:, cols])
 
-        g_bf = [sb.tile([P, N, PACK], BF16, name=f"g_bf{g}", align_bytes=64) for g in range(PASSES)]
+        g_bf = [sb.tile([P, N, PACK], BF16, name=f"g_bf{g}", tag=f"g_bf{g}", align_bytes=64) for g in range(PASSES)]
         g_codes = [sb.tile([P, N], U32, name=f"g_codes{g}", align_bytes=64) for g in range(PASSES)]
         g_scales = [sb.tile([P, N], U8, name=f"g_scales{g}", align_bytes=64) for g in range(PASSES)]
 
@@ -165,24 +177,34 @@ def tile_attend_gkl_w_kernel(tc, xT, wT, y, wt, xm, offs, out):
                 in_=g_bf[g][:, half, :].rearrange("p n t -> p (n t)"),
             )
 
-        coef = sb.tile([P, PACK], F32, name="coef")
-        yw = sb.tile([P, PACK, N], F32, name="yw")
-        g_planes = sb.tile([P, PACK, N], BF16, name="g_planes")
+        coef_head = sb.tile([P, 2], F32, name="coef_head")
+        coef_tail = sb.tile([P, 2], F32, name="coef_tail", tag="x_scales1", align_bytes=64)
+        y_part = sb.tile([P, 2, PACK, HALF], F32, name="y_part", tag="cast1", align_bytes=64)
+        e_part = sb.tile([P, 2, PACK, HALF], F32, name="e_part")
+
+        def by_half(ap):
+            return ap.rearrange("p (h n) -> p h n", n=HALF)
 
         def weigh_y(t):
-            scale_rows(yw[:, t, :], y_raw[:, t, :], wt_sb[:, 0, t : t + 1])
-
-        def coefs(t0, t1):
-            nc.vector.tensor_tensor(out=coef[:, t0:t1], in0=inv[:, t0:t1], in1=wt_sb[:, 0, t0:t1], op=ALU.mult)
-
-        def grad_plane(t):
-            nc.vector.scalar_tensor_tensor(
-                out=g_planes[:, t, :], in0=e_sb[0][:, t, :], scalar=coef[:, t : t + 1], in1=yw[:, t, :],
-                op0=ALU.mult, op1=ALU.subtract,
+            nc.gpsimd.tensor_scalar(
+                out=y_part[:, :, t, :], in0=by_half(y_raw[:, t, :]), scalar1=wt_sb[:, 0, t : t + 1], scalar2=0.0,
+                op0=ALU.mult, op1=ALU.add,
             )
 
-        def weave_planes(copy, cols):
-            copy(woven_view(g_bf[0][:, cols, :], 4), planes_view(g_planes[:, :, cols], 4))
+        def weigh_e(t):
+            coef = coef_head if t < 2 else coef_tail
+            scale_rows(e_part[:, :, t, :], by_half(e_sb[0][:, t, :]), coef[:, t % 2 : t % 2 + 1])
+
+        def coefs(coef, t0):
+            nc.vector.tensor_tensor(out=coef[:], in0=inv[:, t0 : t0 + 2], in1=wt_sb[:, 0, t0 : t0 + 2], op=ALU.mult)
+
+        def grad_parts(half):
+            nc.vector.tensor_tensor(
+                out=woven_view(g_bf[0][:, half, :], 2),
+                in0=planes_view(e_part[:, half.start // HALF], 2),
+                in1=planes_view(y_part[:, half.start // HALF], 2),
+                op=ALU.subtract,
+            )
 
         neg_wt = sb.tile([P, PACK], F32, name="neg_wt")
         neg_coef = sb.tile([P, PACK], F32, name="neg_coef")
@@ -203,39 +225,36 @@ def tile_attend_gkl_w_kernel(tc, xT, wT, y, wt, xm, offs, out):
                 op=ALU.mult,
             )
 
-        m_head = sb.tile([P, HEAD_PIECES, P, PACK], BF16, name="m_head", align_bytes=64)
-        m_tail = sb.tile([P, PIECES - HEAD_PIECES, P, PACK], BF16, name="m_tail", tag="excess", align_bytes=64)
-        m_codes = sb.tile([P, CHUNKS * PASSES * P], U32, name="m_codes", align_bytes=64)
-        m_scales = sb.tile([P, CHUNKS * PASSES * P], U8, name="m_scales", align_bytes=64)
-        res_early = [sb.tile([P, HALF], F32, name=f"res_early{c}") for c in range(CHUNKS)]
+        def piece(c, g):
+            return PASSES * g + c if c < 2 else PASSES * c + g
+
+        m_head = sb.tile([P, HEAD_PIECES * K_PASS], BF16, name="m_head", tag="e_sb0", align_bytes=64)
+        m_tail = sb.tile([P, (PIECES - HEAD_PIECES) * K_PASS], BF16, name="m_tail", align_bytes=64)
+        codes_head = sb.tile([P, 2 * PASSES * P], U32, name="codes_head", align_bytes=64)
+        codes_tail = sb.tile([P, 2 * PASSES * P], U32, name="codes_tail", tag="g_bf1", align_bytes=64)
+        m_scales = sb.tile([P, PIECES * P], U8, name="m_scales", align_bytes=64)
+        res_first = sb.tile([P, 2, HALF], F32, name="res_first", tag="m_raw3")
+        res_early = [res_first[:, 0], res_first[:, 1]] + [sb.tile([P, HALF], F32, name=f"res_early{c}")[:] for c in (2, 3)]
         res_late = [sb.tile([P, HALF], F32, name=f"res_late{c}") for c in range(CHUNKS)]
 
-        def m_bf(c, g0, g1):
-            first = PASSES * c + g0
+        def m_bf(first, count):
             if first < HEAD_PIECES:
-                return m_head[:, first : first + g1 - g0]
-            return m_tail[:, first - HEAD_PIECES : first - HEAD_PIECES + g1 - g0]
+                return m_head[:, K_PASS * first : K_PASS * (first + count)]
+            return m_tail[:, K_PASS * (first - HEAD_PIECES) : K_PASS * (first - HEAD_PIECES + count)]
 
-        def cast_m(copy, c, g0=0, g1=PASSES):
-            h, k = divmod(c, CHUNKS // 2)
+        def cast_chunk(copy, c):
             copy(
-                m_bf(c, g0, g1).rearrange("p g (c i) t -> p g c t i", i=4),
-                m_raw[h][:, g0:g1, :, P * k : P * (k + 1)].rearrange("p g t (c i) -> p g c t i", i=4),
+                m_bf(piece(c, 0), PASSES).rearrange("p (g c i t) -> p g c t i", g=PASSES, i=4, t=PACK),
+                m_raw[c][:].rearrange("p g t (c i) -> p g c t i", i=4),
             )
 
-        def cast_m_pass(g):
-            scopy(
-                m_head[:, g : 2 * PASSES : PASSES].rearrange("p k (c i) t -> p k c t i", i=4),
-                m_raw[0][:, g].rearrange("p t (k c i) -> p k c t i", k=2, i=4),
-            )
+        def m_codes(first, count):
+            tile, place = (codes_head, first) if first < 2 * PASSES else (codes_tail, first - 2 * PASSES)
+            return tile[:, P * place : P * (place + count)].bitcast(E4)
 
-        def quant_m(c, g0=0, g1=PASSES):
-            cols = slice(P * (PASSES * c + g0), P * (PASSES * c + g1))
-            nc.vector.quantize_mx(
-                out=m_codes[:, cols].bitcast(E4),
-                scales=m_scales[:, cols],
-                in_=m_bf(c, g0, g1).rearrange("p g d t -> p (g d t)"),
-            )
+        def quant_m(first, count):
+            cols = slice(P * first, P * (first + count))
+            nc.vector.quantize_mx(out=m_codes(first, count), scales=m_scales[:, cols], in_=m_bf(first, count))
 
         def bank():
             return psum.tile([P, N], F32, name="acc_out", tag="bank")
@@ -243,10 +262,10 @@ def tile_attend_gkl_w_kernel(tc, xT, wT, y, wt, xm, offs, out):
         def product(c, slots, acc):
             order = [1, 0] if c > 0 and slots != early else [0, 1]
             for g in order:
-                cols = slice(P * (PASSES * c + g), P * (PASSES * c + g + 1))
+                cols = slice(P * piece(c, g), P * (piece(c, g) + 1))
                 nc.tensor.matmul_mx(
                     out=acc[:, slots],
-                    lhsT=m_codes[:, cols].bitcast(E4),
+                    lhsT=m_codes(piece(c, g), 1),
                     lhsT_scale=m_scales[:, cols],
                     rhs=g_codes[g][:, slots].bitcast(E5),
                     rhs_scale=g_scales[g][:, slots],
@@ -259,7 +278,7 @@ def tile_attend_gkl_w_kernel(tc, xT, wT, y, wt, xm, offs, out):
             return offsets[:, slots.start // 16 : slots.stop // 16]
 
         def scatter_early(c):
-            nc.scalar.activation(out=windows[c][:].indirect(entries(early)), in_=res_early[c][:], func=ACT.Copy)
+            nc.scalar.activation(out=windows[c][:].indirect(entries(early)), in_=res_early[c], func=ACT.Copy)
 
         def scatter_late(c):
             vcopy(windows[c][:].indirect(entries(late)), res_late[c][:])
@@ -267,65 +286,59 @@ def tile_attend_gkl_w_kernel(tc, xT, wT, y, wt, xm, offs, out):
         def store(c):
             nc.sync.dma_start(out=out[P * c : P * (c + 1), :], in_=windows[c][:])
 
-        weigh_y(0)
-        weigh_y(1)
         scores(0, 0)
         scores(0, 1)
         scores(0, 2)
         scores(0, 3)
-        weigh_y(2)
-        weigh_y(3)
-        cast_m_pass(0)
-        cast_x(vcopy, 1, 0, 2)
+        every = slice(0, N)
         recip(0, 0, 2)
-        cast_x(vcopy, 1, 2, 4)
         quant_x(1, 0, 2)
-        coefs(0, 2)
+        coefs(coef_head, 0)
         quant_x(1, 2, 4)
+        for t in range(PACK):
+            weigh_y(t)
+        weigh_e(0)
+        weigh_e(1)
         for t in range(PACK):
             scores(1, t)
         recip(0, 2, 4)
-        grad_plane(0)
-        coefs(2, 4)
-        for t in range(1, PACK):
-            grad_plane(t)
-
-        every = slice(0, N)
-        cast_m_pass(1)
-        weave_planes(scopy, early)
-        weave_planes(scopy, late)
-        cast_m(scopy, 2)
-        recip(1, 0, PACK)
         excess_plane(0, every)
-        nc.vector.tensor_tensor(out=neg_coef[:], in0=inv[:, PACK : 2 * PACK], in1=neg_wt[:], op=ALU.mult)
+        coefs(coef_tail, 2)
+        weigh_e(2)
+        weigh_e(3)
+        for g in range(PASSES):
+            scopy(woven_view(m_bf(2 * g, 2).rearrange("p (d t) -> p d t", t=PACK), 4), planes_view(m_first[:, g], 4))
+        cast_chunk(scopy, 2)
+        cast_chunk(scopy, 3)
         excess_plane(1, every)
-        excess_plane(2, early)
-        excess_plane(3, early)
-        quant_m(0, 0, 2 * PASSES)
+        excess_plane(2, every)
+        recip(1, 0, PACK)
+        excess_plane(3, every)
+        nc.vector.tensor_tensor(out=neg_coef[:], in0=inv[:, PACK : 2 * PACK], in1=neg_wt[:], op=ALU.mult)
+        grad_parts(early)
         grad_woven(early)
         quant_g(0, early)
+        quant_m(0, 2 * PASSES)
         quant_g(1, early)
-        excess_plane(2, late)
-        excess_plane(3, late)
         for c in (0, 1):
-            scopy(res_early[c][:], product(c, early, bank()))
+            scopy(res_early[c], product(c, early, bank()))
         for c in (0, 1):
             scatter_early(c)
-        quant_g(0, late)
+        grad_parts(late)
         grad_woven(late)
-        quant_m(2)
+        quant_g(0, late)
         quant_g(1, late)
-        cast_m(vcopy, 3)
+        quant_m(piece(2, 0), PASSES)
         vcopy(res_late[0][:], product(0, late, bank()))
         scatter_late(0)
         store(0)
+        quant_m(piece(3, 0), PASSES)
         vcopy(res_late[1][:], product(1, late, bank()))
-        quant_m(3)
         scatter_late(1)
         store(1)
         for c in (2, 3):
             acc = product(c, every, bank())
-            scopy(res_early[c][:], acc[:, early])
+            scopy(res_early[c], acc[:, early])
             scopy(res_late[c][:], acc[:, late])
             scatter_early(c)
             scatter_late(c)

@@ -8,7 +8,7 @@ K_PASS = P * PACK
 PASSES = R // K_PASS
 CHUNKS = D // P
 PIECES = CHUNKS * PASSES
-HEAD_PIECES = 6
+HEAD_PIECES = 4
 HALF = N // 2
 FLOPS = 2 * 2 * D * R * N
 
@@ -57,8 +57,7 @@ def tile_attend_gkl_w_kernel(tc, xT, wT, y, wt, xm, offs, out):
         w_raw = [sb.tile([P, T], F32, name=f"w_raw{j}") for j in range(PACK)]
         y_raw = sb.tile([P, PACK, N], F32, name="y_raw")
         y_tail = sb.tile([P, PACK, N], F32, name="y_tail")
-        m_first = sb.tile([P, PASSES, PACK, D // 2], F32, name="m_first")
-        m_raw = {c: sb.tile([P, PASSES, PACK, P], F32, name=f"m_raw{c}", tag=f"m_raw{c}") for c in (2, 3)}
+        m_raw = [sb.tile([P, PASSES, PACK, D // 2], F32, name=f"m_raw{h}", tag=f"m_raw{h}") for h in range(2)]
         wt_sb = sb.tile([P, PASSES, 8], F32, name="wt_sb")
         windows = [sb.tile([P, T], F32, name=f"window{c}") for c in range(CHUNKS)]
 
@@ -71,8 +70,8 @@ def tile_attend_gkl_w_kernel(tc, xT, wT, y, wt, xm, offs, out):
         def load_y(t0, t1):
             nc.sync.dma_start(out=y_raw[:, t0:t1, :], in_=rows(y, 0)[:, t0:t1, :])
 
-        def load_m(g):
-            nc.sync.dma_start(out=m_first[:, g, :, :], in_=rows(xm, g)[:, :, : D // 2])
+        def load_m(h, g):
+            nc.sync.dma_start(out=m_raw[h][:, g, :, :], in_=rows(xm, g)[:, :, D // 2 * h : D // 2 * (h + 1)])
 
         nc.sync.dma_start(out=w_raw[0][:], in_=w_planes[:, 0, :])
         nc.sync.dma_start(offsets[:], offs)
@@ -87,11 +86,9 @@ def tile_attend_gkl_w_kernel(tc, xT, wT, y, wt, xm, offs, out):
         load_y(0, 2)
         load_y(2, 4)
         nc.sync.dma_start(out=y_tail[:], in_=rows(y, 1))
-        load_m(0)
-        load_m(1)
-        for c in (2, 3):
+        for h in range(2):
             for g in range(PASSES):
-                nc.sync.dma_start(out=m_raw[c][:, g, :, :], in_=rows(xm, g)[:, :, P * c : P * (c + 1)])
+                load_m(h, g)
 
         nc.vector.memset(windows[0][:], 0.0)
         nc.vector.memset(windows[1][:], 0.0)
@@ -185,10 +182,10 @@ def tile_attend_gkl_w_kernel(tc, xT, wT, y, wt, xm, offs, out):
         def by_half(ap):
             return ap.rearrange("p (h n) -> p h n", n=HALF)
 
-        def weigh_y(t):
+        def weigh_y(t, halves):
             nc.gpsimd.tensor_scalar(
-                out=y_part[:, :, t, :], in0=by_half(y_raw[:, t, :]), scalar1=wt_sb[:, 0, t : t + 1], scalar2=0.0,
-                op0=ALU.mult, op1=ALU.add,
+                out=y_part[:, :halves, t, :], in0=by_half(y_raw[:, t, : HALF * halves]), scalar1=wt_sb[:, 0, t : t + 1],
+                scalar2=0.0, op0=ALU.mult, op1=ALU.add,
             )
 
         def weigh_e(t):
@@ -231,9 +228,9 @@ def tile_attend_gkl_w_kernel(tc, xT, wT, y, wt, xm, offs, out):
         m_head = sb.tile([P, HEAD_PIECES * K_PASS], BF16, name="m_head", tag="e_sb0", align_bytes=64)
         m_tail = sb.tile([P, (PIECES - HEAD_PIECES) * K_PASS], BF16, name="m_tail", align_bytes=64)
         codes_head = sb.tile([P, 2 * PASSES * P], U32, name="codes_head", align_bytes=64)
-        codes_tail = sb.tile([P, 2 * PASSES * P], U32, name="codes_tail", tag="g_bf1", align_bytes=64)
+        codes_tail = sb.tile([P, 2 * PASSES * P], U32, name="codes_tail", tag="g_bf0", align_bytes=64)
         m_scales = sb.tile([P, PIECES * P], U8, name="m_scales", align_bytes=64)
-        res_first = sb.tile([P, 2, HALF], F32, name="res_first", tag="m_raw3")
+        res_first = sb.tile([P, 2, HALF], F32, name="res_first", tag="m_raw1")
         res_early = [res_first[:, 0], res_first[:, 1]] + [sb.tile([P, HALF], F32, name=f"res_early{c}")[:] for c in (2, 3)]
         res_late = [sb.tile([P, HALF], F32, name=f"res_late{c}") for c in range(CHUNKS)]
 
@@ -241,12 +238,6 @@ def tile_attend_gkl_w_kernel(tc, xT, wT, y, wt, xm, offs, out):
             if first < HEAD_PIECES:
                 return m_head[:, K_PASS * first : K_PASS * (first + count)]
             return m_tail[:, K_PASS * (first - HEAD_PIECES) : K_PASS * (first - HEAD_PIECES + count)]
-
-        def cast_chunk(copy, c):
-            copy(
-                m_bf(piece(c, 0), PASSES).rearrange("p (g c i t) -> p g c t i", g=PASSES, i=4, t=PACK),
-                m_raw[c][:].rearrange("p g t (c i) -> p g c t i", i=4),
-            )
 
         def m_codes(first, count):
             tile, place = (codes_head, first) if first < 2 * PASSES else (codes_tail, first - 2 * PASSES)
@@ -260,7 +251,7 @@ def tile_attend_gkl_w_kernel(tc, xT, wT, y, wt, xm, offs, out):
             return psum.tile([P, N], F32, name="acc_out", tag="bank")
 
         def product(c, slots, acc):
-            order = [1, 0] if c > 0 and slots != early else [0, 1]
+            order = [1, 0] if (c, slots) == (0, late) else [0, 1]
             for g in order:
                 cols = slice(P * piece(c, g), P * (piece(c, g) + 1))
                 nc.tensor.matmul_mx(
@@ -295,8 +286,9 @@ def tile_attend_gkl_w_kernel(tc, xT, wT, y, wt, xm, offs, out):
         quant_x(1, 0, 2)
         coefs(coef_head, 0)
         quant_x(1, 2, 4)
-        for t in range(PACK):
-            weigh_y(t)
+        for t in range(PACK - 1):
+            weigh_y(t, 2)
+        weigh_y(PACK - 1, 1)
         weigh_e(0)
         weigh_e(1)
         for t in range(PACK):
@@ -307,9 +299,12 @@ def tile_attend_gkl_w_kernel(tc, xT, wT, y, wt, xm, offs, out):
         weigh_e(2)
         weigh_e(3)
         for g in range(PASSES):
-            scopy(woven_view(m_bf(2 * g, 2).rearrange("p (d t) -> p d t", t=PACK), 4), planes_view(m_first[:, g], 4))
-        cast_chunk(scopy, 2)
-        cast_chunk(scopy, 3)
+            scopy(woven_view(m_bf(2 * g, 2).rearrange("p (d t) -> p d t", t=PACK), 4), planes_view(m_raw[0][:, g], 4))
+        for g in range(PASSES):
+            scopy(
+                m_tail[:].rearrange("p (k g c i t) -> p g k c t i", k=2, g=PASSES, i=4, t=PACK)[:, g],
+                m_raw[1][:, g].rearrange("p t (k c i) -> p k c t i", k=2, i=4),
+            )
         excess_plane(1, every)
         excess_plane(2, every)
         recip(1, 0, PACK)
@@ -324,10 +319,14 @@ def tile_attend_gkl_w_kernel(tc, xT, wT, y, wt, xm, offs, out):
             scopy(res_early[c], product(c, early, bank()))
         for c in (0, 1):
             scatter_early(c)
-        grad_parts(late)
+        nc.vector.tensor_scalar(
+            out=y_part[:, 1, PACK - 1, :], in0=y_raw[:, PACK - 1, late], scalar1=wt_sb[:, 0, PACK - 1 : PACK], scalar2=None,
+            op0=ALU.mult,
+        )
         grad_woven(late)
-        quant_g(0, late)
+        grad_parts(late)
         quant_g(1, late)
+        quant_g(0, late)
         quant_m(piece(2, 0), PASSES)
         vcopy(res_late[0][:], product(0, late, bank()))
         scatter_late(0)

@@ -299,11 +299,11 @@ def tile_attend_gkl_w_kernel(tc, xT, wT, y, wt, xm, offs, out):
         weigh_e(2)
         weigh_e(3)
         for g in range(PASSES):
-            scopy(woven_view(m_bf(2 * g, 2).rearrange("p (d t) -> p d t", t=PACK), 4), planes_view(m_raw[0][:, g], 4))
+            scopy(woven_view(m_bf(2 * g, 2).rearrange("p (d t) -> p d t", t=PACK), 2), planes_view(m_raw[0][:, g], 2))
         for g in range(PASSES):
             scopy(
-                m_tail[:].rearrange("p (k g c i t) -> p g k c t i", k=2, g=PASSES, i=4, t=PACK)[:, g],
-                m_raw[1][:, g].rearrange("p t (k c i) -> p k c t i", k=2, i=4),
+                m_tail[:].rearrange("p (k g c i t) -> p g k c t i", k=2, g=PASSES, i=2, t=PACK)[:, g],
+                m_raw[1][:, g].rearrange("p t (k c i) -> p k c t i", k=2, i=2),
             )
         excess_plane(1, every)
         excess_plane(2, every)

@@ -52,7 +52,7 @@ def tile_attend_gkl_w_kernel(tc, xT, wT, y, wt, xm, offs, out):
         psum = ctx.enter_context(tc.psum_pool(name="psum", bufs=8))
 
         offsets = held.tile([P, N // 16], U16, name="offsets")
-        x_head = [sb.tile([P, PACK, K_PASS // 2], F32, name=f"x_head{h}") for h in range(2)]
+        x_head = sb.tile([P, PACK, K_PASS], F32, name="x_head")
         x_tail = [sb.tile([P, PACK, K_PASS // 2], F32, name=f"x_tail{h}") for h in range(2)]
         w_raw = [sb.tile([P, T], F32, name=f"w_raw{j}") for j in range(PACK)]
         y_raw = sb.tile([P, PACK, N], F32, name="y_raw")
@@ -77,8 +77,7 @@ def tile_attend_gkl_w_kernel(tc, xT, wT, y, wt, xm, offs, out):
         nc.sync.dma_start(offsets[:], offs)
         for j in range(1, PACK):
             nc.sync.dma_start(out=w_raw[j][:], in_=w_planes[:, j, :])
-        for h in range(2):
-            nc.sync.dma_start(out=x_head[h][:], in_=x_planes[:, :, K_PASS // 2 * h : K_PASS // 2 * (h + 1)])
+        nc.sync.dma_start(out=x_head[:], in_=x_planes[:, :, 0:K_PASS])
         for h in range(2):
             first = K_PASS + K_PASS // 2 * h
             nc.sync.dma_start(out=x_tail[h][:], in_=x_planes[:, :, first : first + K_PASS // 2])
@@ -95,13 +94,20 @@ def tile_attend_gkl_w_kernel(tc, xT, wT, y, wt, xm, offs, out):
         nc.vector.memset(windows[2][:], 0.0)
         nc.gpsimd.memset(windows[3][:], 0.0)
 
-        x_bf = [sb.tile([P, K_PASS * PACK], BF16, name=f"x_bf{g}", tag=f"cast{g}", align_bytes=64) for g in range(PASSES)]
+        x_pair = [sb.tile([P, 2 * K_PASS], BF16, name=f"x_pair{u}", tag=f"x_pair{u}", align_bytes=64) for u in range(2)]
+        x_last = sb.tile([P, K_PASS * PACK], BF16, name="x_last", tag="cast1", align_bytes=64)
+
+        def x_bf(g, t0, t1):
+            if g == 0:
+                return x_pair[t0 // 2][:, K_PASS * (t0 % 2) : K_PASS * (t0 % 2 + t1 - t0)]
+            return x_last[:, K_PASS * t0 : K_PASS * t1]
+
         x_codes = [sb.tile([P, K_PASS], U32, name=f"x_codes{g}", align_bytes=64) for g in range(PASSES)]
         x_scales = [sb.tile([P, K_PASS], U8, name=f"x_scales{g}", tag=f"x_scales{g}", align_bytes=64) for g in range(PASSES)]
 
         def cast_x(copy, g, t0, t1, raw, m0, m1):
             copy(
-                x_bf[g][:].rearrange("p (t m j) -> p m j t", t=PACK, j=PACK)[:, m0:m1, :, t0:t1],
+                x_bf(g, t0, t1).rearrange("p (t m j) -> p m j t", t=t1 - t0, j=PACK)[:, m0:m1],
                 raw[:].rearrange("p j (m t) -> p m j t", t=PACK)[:, :, :, t0:t1],
             )
 
@@ -109,7 +115,7 @@ def tile_attend_gkl_w_kernel(tc, xT, wT, y, wt, xm, offs, out):
             nc.vector.quantize_mx(
                 out=x_codes[g][:, P * t0 : P * t1].bitcast(E4),
                 scales=x_scales[g][:, P * t0 : P * t1],
-                in_=x_bf[g][:, P * PACK * t0 : P * PACK * t1],
+                in_=x_bf(g, t0, t1),
             )
 
         w_bf = sb.tile([P, N, PACK], BF16, name="w_bf", align_bytes=64)
@@ -123,20 +129,18 @@ def tile_attend_gkl_w_kernel(tc, xT, wT, y, wt, xm, offs, out):
             nc.vector.quantize_mx(
                 out=w_codes[:, half].bitcast(E4), scales=w_scales[:, half], in_=w_bf[:, half, :].rearrange("p n j -> p (n j)")
             )
-        cast_x(scopy, 0, 0, 2, x_head[0], 0, P // 2)
-        cast_x(scopy, 0, 2, 4, x_head[0], 0, P // 2)
-        cast_x(vcopy, 0, 0, 2, x_head[1], P // 2, P)
+        cast_x(vcopy, 0, 0, 2, x_head, 0, P)
+        cast_x(scopy, 0, 2, 4, x_head, 0, P)
         quant_x(0, 0, 1)
-        cast_x(vcopy, 0, 2, 4, x_head[1], P // 2, P)
         quant_x(0, 1, 2)
         quant_x(0, 2, 4)
         cast_x(scopy, 1, 0, 4, x_tail[0], 0, P // 2)
         gcopy(
-            x_bf[1][:].rearrange("p (t m j) -> p m t j", t=PACK, j=PACK)[:, P // 2 :],
+            x_last[:].rearrange("p (t m j) -> p m t j", t=PACK, j=PACK)[:, P // 2 :],
             x_tail[1][:].rearrange("p j (m t) -> p m t j", t=PACK),
         )
 
-        neg_max = sb.tile([P, PASSES * PACK], F32, name="neg_max")
+        neg_max = sb.tile([P, PASSES * PACK], F32, name="neg_max", tag="x_pair1", align_bytes=64)
         sums = sb.tile([P, PASSES * PACK], F32, name="sums")
         inv = sb.tile([P, PASSES * PACK], F32, name="inv")
         e_sb = [sb.tile([P, PACK, N], F32, name=f"e_sb{g}", tag=f"e_sb{g}", align_bytes=64) for g in range(PASSES)]
@@ -159,8 +163,8 @@ def tile_attend_gkl_w_kernel(tc, xT, wT, y, wt, xm, offs, out):
                 out=e_sb[g][:, t, :], in_=acc[:], func=ACT.Exp, bias=neg_max[:, i : i + 1], accum_out=sums[:, i : i + 1]
             )
 
-        def recip(g, t0, t1):
-            cols = slice(PACK * g + t0, PACK * g + t1)
+        def recip(first, last):
+            cols = slice(first, last)
             nc.vector.reciprocal(out=inv[:, cols], in_=sums[:, cols])
 
         g_bf = [sb.tile([P, N, PACK], BF16, name=f"g_bf{g}", tag=f"g_bf{g}", align_bytes=64) for g in range(PASSES)]
@@ -282,7 +286,7 @@ def tile_attend_gkl_w_kernel(tc, xT, wT, y, wt, xm, offs, out):
         scores(0, 2)
         scores(0, 3)
         every = slice(0, N)
-        recip(0, 0, 2)
+        recip(0, 2)
         quant_x(1, 0, 2)
         coefs(coef_head, 0)
         quant_x(1, 2, 4)
@@ -293,7 +297,7 @@ def tile_attend_gkl_w_kernel(tc, xT, wT, y, wt, xm, offs, out):
         weigh_e(1)
         for t in range(PACK):
             scores(1, t)
-        recip(0, 2, 4)
+        recip(2, 6)
         excess_plane(0, every)
         coefs(coef_tail, 2)
         weigh_e(2)
@@ -307,7 +311,7 @@ def tile_attend_gkl_w_kernel(tc, xT, wT, y, wt, xm, offs, out):
             )
         excess_plane(1, every)
         excess_plane(2, every)
-        recip(1, 0, PACK)
+        recip(6, 8)
         excess_plane(3, every)
         nc.vector.tensor_tensor(out=neg_coef[:], in0=inv[:, PACK : 2 * PACK], in1=neg_wt[:], op=ALU.mult)
         grad_parts(early)

@@ -84,7 +84,8 @@ def tile_attend_gkl_w_kernel(tc, xT, wT, y, wt, xm, offs, out):
         nc.sync.dma_start(out=wt_sb[:, :, 0:PACK], in_=wt[0].rearrange("(g p t) o -> p g (t o)", g=PASSES, t=PACK))
         load_y(0, 2)
         load_y(2, 4)
-        nc.sync.dma_start(out=y_tail[:], in_=rows(y, 1))
+        for t in (0, 2):
+            nc.sync.dma_start(out=y_tail[:, t : t + 2, :], in_=rows(y, 1)[:, t : t + 2, :])
         for h in range(2):
             for g in range(PASSES):
                 load_m(h, g)
@@ -186,9 +187,9 @@ def tile_attend_gkl_w_kernel(tc, xT, wT, y, wt, xm, offs, out):
         def by_half(ap):
             return ap.rearrange("p (h n) -> p h n", n=HALF)
 
-        def weigh_y(t, halves):
+        def weigh_y(t):
             nc.gpsimd.tensor_scalar(
-                out=y_part[:, :halves, t, :], in0=by_half(y_raw[:, t, : HALF * halves]), scalar1=wt_sb[:, 0, t : t + 1],
+                out=y_part[:, :, t, :], in0=by_half(y_raw[:, t, :]), scalar1=wt_sb[:, 0, t : t + 1],
                 scalar2=0.0, op0=ALU.mult, op1=ALU.add,
             )
 
@@ -290,9 +291,11 @@ def tile_attend_gkl_w_kernel(tc, xT, wT, y, wt, xm, offs, out):
         quant_x(1, 0, 2)
         coefs(coef_head, 0)
         quant_x(1, 2, 4)
-        for t in range(PACK - 1):
-            weigh_y(t, 2)
-        weigh_y(PACK - 1, 1)
+        nc.vector.tensor_scalar(
+            out=y_part[:, :, 0, :], in0=by_half(y_raw[:, 0, :]), scalar1=wt_sb[:, 0, 0:1], scalar2=None, op0=ALU.mult
+        )
+        for t in range(1, PACK):
+            weigh_y(t)
         weigh_e(0)
         weigh_e(1)
         for t in range(PACK):
@@ -323,10 +326,6 @@ def tile_attend_gkl_w_kernel(tc, xT, wT, y, wt, xm, offs, out):
             scopy(res_early[c], product(c, early, bank()))
         for c in (0, 1):
             scatter_early(c)
-        nc.vector.tensor_scalar(
-            out=y_part[:, 1, PACK - 1, :], in0=y_raw[:, PACK - 1, late], scalar1=wt_sb[:, 0, PACK - 1 : PACK], scalar2=None,
-            op0=ALU.mult,
-        )
         grad_woven(late)
         grad_parts(late)
         quant_g(1, late)

@@ -84,8 +84,7 @@ def tile_attend_gkl_w_kernel(tc, xT, wT, y, wt, xm, offs, out):
         nc.sync.dma_start(out=wt_sb[:, :, 0:PACK], in_=wt[0].rearrange("(g p t) o -> p g (t o)", g=PASSES, t=PACK))
         load_y(0, 2)
         load_y(2, 4)
-        for t in (0, 2):
-            nc.sync.dma_start(out=y_tail[:, t : t + 2, :], in_=rows(y, 1)[:, t : t + 2, :])
+        nc.sync.dma_start(out=y_tail[:], in_=rows(y, 1))
         for h in range(2):
             for g in range(PASSES):
                 load_m(h, g)

@@ -207,10 +207,8 @@ def tile_attend_gkl_w_kernel(tc, xT, wT, y, wt, xm, offs, out):
                 op=ALU.subtract,
             )
 
-        neg_wt = sb.tile([P, PACK], F32, name="neg_wt")
         neg_coef = sb.tile([P, PACK], F32, name="neg_coef")
         excess = sb.tile([P, PACK, N], F32, name="excess", tag="excess", align_bytes=64)
-        scale_rows(neg_wt[:], wt_sb[:, 1, 0:PACK], -1.0)
 
         def excess_plane(t, half):
             nc.vector.scalar_tensor_tensor(
@@ -315,7 +313,9 @@ def tile_attend_gkl_w_kernel(tc, xT, wT, y, wt, xm, offs, out):
         excess_plane(2, every)
         recip(6, 8)
         excess_plane(3, every)
-        nc.vector.tensor_tensor(out=neg_coef[:], in0=inv[:, PACK : 2 * PACK], in1=neg_wt[:], op=ALU.mult)
+        nc.vector.scalar_tensor_tensor(
+            out=neg_coef[:], in0=inv[:, PACK : 2 * PACK], scalar=-1.0, in1=wt_sb[:, 1, 0:PACK], op0=ALU.mult, op1=ALU.mult
+        )
         grad_parts(early)
         grad_woven(early)
         quant_g(0, early)

@@ -89,10 +89,8 @@ def tile_attend_gkl_w_kernel(tc, xT, wT, y, wt, xm, offs, out):
             for g in range(PASSES):
                 load_m(h, g)
 
-        nc.vector.memset(windows[0][:], 0.0)
-        nc.vector.memset(windows[1][:], 0.0)
-        nc.vector.memset(windows[2][:], 0.0)
-        nc.gpsimd.memset(windows[3][:], 0.0)
+        for window in windows:
+            nc.vector.memset(window[:], 0.0)
 
         x_pair = [sb.tile([P, 2 * K_PASS], BF16, name=f"x_pair{u}", tag=f"x_pair{u}", align_bytes=64) for u in range(2)]
         x_last = sb.tile([P, K_PASS * PACK], BF16, name="x_last", tag="cast1", align_bytes=64)

from contextlib import ExitStack

import concourse.mybir as mybir

D, T, R, N = 512, 2048, 1024, 512
P, PACK = 128, 4
K_PASS = P * PACK
PASSES = R // K_PASS
CHUNKS = D // P
PIECES = CHUNKS * PASSES
HEAD_PIECES = 4
HALF = N // 2
FLOPS = 2 * 2 * D * R * N

F32 = mybir.dt.float32
BF16 = mybir.dt.bfloat16
U32 = mybir.dt.uint32
U16 = mybir.dt.uint16
U8 = mybir.dt.uint8
E4 = mybir.dt.float8_e4m3fn_x4
E5 = mybir.dt.float8_e5m2_x4
ALU = mybir.AluOpType
ACT = mybir.ActivationFunctionType
AX = mybir.AxisListType


def tile_attend_gkl_w_kernel(tc, xT, wT, y, wt, xm, offs, out):
    nc = tc.nc
    early, late = slice(0, HALF), slice(HALF, N)

    def vcopy(dst, src):
        nc.vector.tensor_copy(out=dst, in_=src)

    def scopy(dst, src):
        nc.scalar.copy(out=dst, in_=src)

    def gcopy(dst, src):
        nc.gpsimd.tensor_scalar(out=dst, in0=src, scalar1=1.0, scalar2=0.0, op0=ALU.mult, op1=ALU.add)

    def scale_rows(dst, src, factor):
        nc.scalar.activation(out=dst, in_=src, func=ACT.Copy, scale=factor)

    def woven_view(ap, run):
        return ap.rearrange("p (c i) t -> p c t i", i=run)

    def planes_view(ap, run):
        return ap.rearrange("p t (c i) -> p c t i", i=run)

    with ExitStack() as ctx:
        held = ctx.enter_context(tc.tile_pool(name="held", bufs=1))
        sb = ctx.enter_context(tc.tile_pool(name="sb", bufs=1))
        psum = ctx.enter_context(tc.psum_pool(name="psum", bufs=8))

        offsets = held.tile([P, N // 16], U16, name="offsets")
        x_head = sb.tile([P, PACK, K_PASS], F32, name="x_head")
        x_tail = [sb.tile([P, PACK, K_PASS // 2], F32, name=f"x_tail{h}") for h in range(2)]
        w_raw = [sb.tile([P, T], F32, name=f"w_raw{j}") for j in range(PACK)]
        y_raw = sb.tile([P, PACK, N], F32, name="y_raw")
        y_tail = sb.tile([P, PACK, N], F32, name="y_tail")
        m_raw = [sb.tile([P, PASSES, PACK, D // 2], F32, name=f"m_raw{h}", tag=f"m_raw{h}") for h in range(2)]
        wt_sb = sb.tile([P, PASSES, 8], F32, name="wt_sb")
        windows = [sb.tile([P, T], F32, name=f"window{c}") for c in range(CHUNKS)]

        x_planes = xT[0].rearrange("(p j) r -> p j r", j=PACK)
        w_planes = wT.rearrange("(p j) c -> p j c", j=PACK)

        def rows(ap, g):
            return ap[0, K_PASS * g : K_PASS * (g + 1), :].rearrange("(p t) n -> p t n", t=PACK)

        def load_y(t0, t1):
            nc.sync.dma_start(out=y_raw[:, t0:t1, :], in_=rows(y, 0)[:, t0:t1, :])

        def load_m(h, g):
            nc.sync.dma_start(out=m_raw[h][:, g, :, :], in_=rows(xm, g)[:, :, D // 2 * h : D // 2 * (h + 1)])

        nc.sync.dma_start(out=w_raw[0][:], in_=w_planes[:, 0, :])
        nc.sync.dma_start(offsets[:], offs)
        for j in range(1, PACK):
            nc.sync.dma_start(out=w_raw[j][:], in_=w_planes[:, j, :])
        nc.sync.dma_start(out=x_head[:], in_=x_planes[:, :, 0:K_PASS])
        for h in range(2):
            first = K_PASS + K_PASS // 2 * h
            nc.sync.dma_start(out=x_tail[h][:], in_=x_planes[:, :, first : first + K_PASS // 2])
        nc.sync.dma_start(out=wt_sb[:, :, 0:PACK], in_=wt[0].rearrange("(g p t) o -> p g (t o)", g=PASSES, t=PACK))
        load_y(0, 2)
        load_y(2, 4)
        nc.sync.dma_start(out=y_tail[:], in_=rows(y, 1))
        for h in range(2):
            for g in range(PASSES):
                load_m(h, g)

        for window in windows:
            nc.vector.memset(window[:], 0.0)

        x_pair = [sb.tile([P, 2 * K_PASS], BF16, name=f"x_pair{u}", tag=f"x_pair{u}", align_bytes=64) for u in range(2)]
        x_last = sb.tile([P, K_PASS * PACK], BF16, name="x_last", tag="cast1", align_bytes=64)

        def x_bf(g, t0, t1):
            if g == 0:
                return x_pair[t0 // 2][:, K_PASS * (t0 % 2) : K_PASS * (t0 % 2 + t1 - t0)]
            return x_last[:, K_PASS * t0 : K_PASS * t1]

        x_codes = [sb.tile([P, K_PASS], U32, name=f"x_codes{g}", align_bytes=64) for g in range(PASSES)]
        x_scales = [sb.tile([P, K_PASS], U8, name=f"x_scales{g}", tag=f"x_scales{g}", align_bytes=64) for g in range(PASSES)]

        def cast_x(copy, g, t0, t1, raw, m0, m1):
            copy(
                x_bf(g, t0, t1).rearrange("p (t m j) -> p m j t", t=t1 - t0, j=PACK)[:, m0:m1],
                raw[:].rearrange("p j (m t) -> p m j t", t=PACK)[:, :, :, t0:t1],
            )

        def quant_x(g, t0, t1):
            nc.vector.quantize_mx(
                out=x_codes[g][:, P * t0 : P * t1].bitcast(E4),
                scales=x_scales[g][:, P * t0 : P * t1],
                in_=x_bf(g, t0, t1),
            )

        w_bf = sb.tile([P, N, PACK], BF16, name="w_bf", align_bytes=64)
        w_codes = sb.tile([P, N], U32, name="w_codes", align_bytes=64)
        w_scales = sb.tile([P, N], U8, name="w_scales", align_bytes=64)
        for j in range(PACK - 1):
            vcopy(w_bf[:, :, j], w_raw[j][:].indirect(offsets[:]))
        for half in (early, late):
            vcopy(w_bf[:, half, PACK - 1], w_raw[PACK - 1][:].indirect(offsets[:, half.start // 16 : half.stop // 16]))
        for half in (early, late):
            nc.vector.quantize_mx(
                out=w_codes[:, half].bitcast(E4), scales=w_scales[:, half], in_=w_bf[:, half, :].rearrange("p n j -> p (n j)")
            )
        cast_x(vcopy, 0, 0, 2, x_head, 0, P)
        cast_x(scopy, 0, 2, 4, x_head, 0, P)
        quant_x(0, 0, 1)
        quant_x(0, 1, 2)
        quant_x(0, 2, 4)
        cast_x(scopy, 1, 0, 4, x_tail[0], 0, P // 2)
        gcopy(
            x_last[:].rearrange("p (t m j) -> p m t j", t=PACK, j=PACK)[:, P // 2 :],
            x_tail[1][:].rearrange("p j (m t) -> p m t j", t=PACK),
        )

        neg_max = sb.tile([P, PASSES * PACK], F32, name="neg_max", tag="x_pair1", align_bytes=64)
        sums = sb.tile([P, PASSES * PACK], F32, name="sums")
        inv = sb.tile([P, PASSES * PACK], F32, name="inv")
        e_sb = [sb.tile([P, PACK, N], F32, name=f"e_sb{g}", tag=f"e_sb{g}", align_bytes=64) for g in range(PASSES)]

        def scores(g, t):
            i = PACK * g + t
            cols = slice(P * t, P * (t + 1))
            acc = psum.tile([P, N], F32, name="acc", tag="bank")
            nc.tensor.matmul_mx(
                out=acc[:],
                lhsT=x_codes[g][:, cols].bitcast(E4),
                lhsT_scale=x_scales[g][:, cols],
                rhs=w_codes[:].bitcast(E4),
                rhs_scale=w_scales[:],
                start=True,
                stop=True,
            )
            nc.vector.tensor_reduce(out=neg_max[:, i : i + 1], in_=acc[:], axis=AX.X, op=ALU.max, negate=True)
            nc.scalar.activation(
                out=e_sb[g][:, t, :], in_=acc[:], func=ACT.Exp, bias=neg_max[:, i : i + 1], accum_out=sums[:, i : i + 1]
            )

        def recip(first, last):
            cols = slice(first, last)
            nc.vector.reciprocal(out=inv[:, cols], in_=sums[:, cols])

        g_bf = [sb.tile([P, N, PACK], BF16, name=f"g_bf{g}", tag=f"g_bf{g}", align_bytes=64) for g in range(PASSES)]
        g_codes = [sb.tile([P, N], U32, name=f"g_codes{g}", align_bytes=64) for g in range(PASSES)]
        g_scales = [sb.tile([P, N], U8, name=f"g_scales{g}", align_bytes=64) for g in range(PASSES)]

        def quant_g(g, half):
            nc.vector.quantize_mx(
                out=g_codes[g][:, half].bitcast(E5),
                scales=g_scales[g][:, half],
                in_=g_bf[g][:, half, :].rearrange("p n t -> p (n t)"),
            )

        coef_head = sb.tile([P, 2], F32, name="coef_head")
        coef_tail = sb.tile([P, 2], F32, name="coef_tail", tag="x_scales1", align_bytes=64)
        y_part = sb.tile([P, 2, PACK, HALF], F32, name="y_part", tag="cast1", align_bytes=64)
        e_part = sb.tile([P, 2, PACK, HALF], F32, name="e_part")

        def by_half(ap):
            return ap.rearrange("p (h n) -> p h n", n=HALF)

        def weigh_y(t):
            nc.gpsimd.tensor_scalar(
                out=y_part[:, :, t, :], in0=by_half(y_raw[:, t, :]), scalar1=wt_sb[:, 0, t : t + 1],
                scalar2=0.0, op0=ALU.mult, op1=ALU.add,
            )

        def weigh_e(t):
            coef = coef_head if t < 2 else coef_tail
            scale_rows(e_part[:, :, t, :], by_half(e_sb[0][:, t, :]), coef[:, t % 2 : t % 2 + 1])

        def coefs(coef, t0):
            nc.vector.tensor_tensor(out=coef[:], in0=inv[:, t0 : t0 + 2], in1=wt_sb[:, 0, t0 : t0 + 2], op=ALU.mult)

        def grad_parts(half):
            nc.vector.tensor_tensor(
                out=woven_view(g_bf[0][:, half, :], 2),
                in0=planes_view(e_part[:, half.start // HALF], 2),
                in1=planes_view(y_part[:, half.start // HALF], 2),
                op=ALU.subtract,
            )

        neg_coef = sb.tile([P, PACK], F32, name="neg_coef")
        excess = sb.tile([P, PACK, N], F32, name="excess", tag="excess", align_bytes=64)

        def excess_plane(t, half):
            nc.vector.scalar_tensor_tensor(
                out=excess[:, t, half], in0=y_tail[:, t, half], scalar=sums[:, PACK + t : PACK + t + 1],
                in1=e_sb[1][:, t, half], op0=ALU.mult, op1=ALU.subtract,
            )

        def grad_woven(half):
            nc.vector.tensor_tensor(
                out=woven_view(g_bf[1][:, half, :], 2),
                in0=planes_view(excess[:, :, half], 2),
                in1=neg_coef[:].unsqueeze(1).unsqueeze(3).to_broadcast([P, (half.stop - half.start) // 2, PACK, 2]),
                op=ALU.mult,
            )

        def piece(c, g):
            return PASSES * g + c if c < 2 else PASSES * c + g

        m_head = sb.tile([P, HEAD_PIECES * K_PASS], BF16, name="m_head", tag="e_sb0", align_bytes=64)
        m_tail = sb.tile([P, (PIECES - HEAD_PIECES) * K_PASS], BF16, name="m_tail", align_bytes=64)
        codes_head = sb.tile([P, 2 * PASSES * P], U32, name="codes_head", align_bytes=64)
        codes_tail = sb.tile([P, 2 * PASSES * P], U32, name="codes_tail", tag="g_bf0", align_bytes=64)
        m_scales = sb.tile([P, PIECES * P], U8, name="m_scales", align_bytes=64)
        res_first = sb.tile([P, 2, HALF], F32, name="res_first", tag="m_raw1")
        res_early = [res_first[:, 0], res_first[:, 1]] + [sb.tile([P, HALF], F32, name=f"res_early{c}")[:] for c in (2, 3)]
        res_late = [sb.tile([P, HALF], F32, name=f"res_late{c}") for c in range(CHUNKS)]

        def m_bf(first, count):
            if first < HEAD_PIECES:
                return m_head[:, K_PASS * first : K_PASS * (first + count)]
            return m_tail[:, K_PASS * (first - HEAD_PIECES) : K_PASS * (first - HEAD_PIECES + count)]

        def m_codes(first, count):
            tile, place = (codes_head, first) if first < 2 * PASSES else (codes_tail, first - 2 * PASSES)
            return tile[:, P * place : P * (place + count)].bitcast(E4)

        def quant_m(first, count):
            cols = slice(P * first, P * (first + count))
            nc.vector.quantize_mx(out=m_codes(first, count), scales=m_scales[:, cols], in_=m_bf(first, count))

        def bank():
            return psum.tile([P, N], F32, name="acc_out", tag="bank")

        def product(c, slots, acc):
            order = [1, 0] if (c, slots) == (0, late) else [0, 1]
            for g in order:
                cols = slice(P * piece(c, g), P * (piece(c, g) + 1))
                nc.tensor.matmul_mx(
                    out=acc[:, slots],
                    lhsT=m_codes(piece(c, g), 1),
                    lhsT_scale=m_scales[:, cols],
                    rhs=g_codes[g][:, slots].bitcast(E5),
                    rhs_scale=g_scales[g][:, slots],
                    start=(g == order[0]),
                    stop=(g == order[-1]),
                )
            return acc[:, slots]

        def entries(slots):
            return offsets[:, slots.start // 16 : slots.stop // 16]

        def scatter_early(c):
            nc.scalar.activation(out=windows[c][:].indirect(entries(early)), in_=res_early[c], func=ACT.Copy)

        def scatter_late(c):
            vcopy(windows[c][:].indirect(entries(late)), res_late[c][:])

        def store(c):
            nc.sync.dma_start(out=out[P * c : P * (c + 1), :], in_=windows[c][:])

        scores(0, 0)
        scores(0, 1)
        scores(0, 2)
        scores(0, 3)
        every = slice(0, N)
        recip(0, 2)
        quant_x(1, 0, 2)
        coefs(coef_head, 0)
        quant_x(1, 2, 4)
        nc.vector.tensor_scalar(
            out=y_part[:, :, 0, :], in0=by_half(y_raw[:, 0, :]), scalar1=wt_sb[:, 0, 0:1], scalar2=None, op0=ALU.mult
        )
        for t in range(1, PACK):
            weigh_y(t)
        weigh_e(0)
        weigh_e(1)
        for t in range(PACK):
            scores(1, t)
        recip(2, 6)
        excess_plane(0, every)
        coefs(coef_tail, 2)
        weigh_e(2)
        weigh_e(3)
        for g in range(PASSES):
            scopy(woven_view(m_bf(2 * g, 2).rearrange("p (d t) -> p d t", t=PACK), 2), planes_view(m_raw[0][:, g], 2))
        for g in range(PASSES):
            scopy(
                m_tail[:].rearrange("p (k g c i t) -> p g k c t i", k=2, g=PASSES, i=2, t=PACK)[:, g],
                m_raw[1][:, g].rearrange("p t (k c i) -> p k c t i", k=2, i=2),
            )
        excess_plane(1, every)
        excess_plane(2, every)
        recip(6, 8)
        excess_plane(3, every)
        nc.vector.scalar_tensor_tensor(
            out=neg_coef[:], in0=inv[:, PACK : 2 * PACK], scalar=-1.0, in1=wt_sb[:, 1, 0:PACK], op0=ALU.mult, op1=ALU.mult
        )
        grad_parts(early)
        grad_woven(early)
        quant_g(0, early)
        quant_m(0, 2 * PASSES)
        quant_g(1, early)
        for c in (0, 1):
            scopy(res_early[c], product(c, early, bank()))
        for c in (0, 1):
            scatter_early(c)
        grad_woven(late)
        grad_parts(late)
        quant_g(1, late)
        quant_g(0, late)
        quant_m(piece(2, 0), PASSES)
        vcopy(res_late[0][:], product(0, late, bank()))
        scatter_late(0)
        store(0)
        quant_m(piece(3, 0), PASSES)
        vcopy(res_late[1][:], product(1, late, bank()))
        scatter_late(1)
        store(1)
        for c in (2, 3):
            acc = product(c, every, bank())
            scopy(res_early[c], acc[:, early])
            scopy(res_late[c][:], acc[:, late])
            scatter_early(c)
            scatter_late(c)
            store(c)
